import numpy as np
import ml_dtypes


def mxq(x, axis, fmt="e4m3"):
    dtype, down = {"e4m3": (ml_dtypes.float8_e4m3fn, 7), "e5m2": (ml_dtypes.float8_e5m2, 14)}[fmt]
    v = np.moveaxis(np.asarray(x, np.float32).astype(ml_dtypes.bfloat16).astype(np.float64), axis, -1)
    blocks = v.reshape(v.shape[:-1] + (-1, 32))
    amax = np.abs(blocks).max(-1, keepdims=True)
    byte = np.maximum(np.where(amax > 0, np.frexp(amax)[1] - 1 + 127, 0) - down, 1)
    scale = np.exp2(byte - 127.0)
    codes = (blocks / scale).astype(np.float32).astype(dtype).astype(np.float64)
    return np.moveaxis((codes * scale).reshape(v.shape), -1, axis)


WIDE = False


def mx_kscale(k):
    if not WIDE:
        return np.ones(k)
    levels = np.array([10, -10, 5, -5, 0])
    if k % 512:
        return np.exp2(np.random.permutation(np.resize(levels, k // 32))).repeat(32)
    a = np.empty((k // 512, 16))
    for p in range(k // 512):
        a[p, :8] = np.random.permutation(np.resize(levels, 8))
        for g in range(8):
            far = levels[np.abs(levels - a[p, g]) >= 10]
            a[p, g + 8] = far[np.random.randint(len(far))]
    return np.exp2(a.ravel()).repeat(32)


BF16 = ml_dtypes.bfloat16


def bf(x):
    return np.asarray(x, np.float32).astype(BF16)


def f64(x):
    return np.asarray(x).astype(np.float64)


E2M1 = np.array([0.0, 0.5, 1.0, 1.5, 2.0, 3.0, 4.0, 6.0, -0.0, -0.5, -1.0, -1.5, -2.0, -3.0, -4.0, -6.0])


def pack_weight(w, fmt):
    k, n = w.shape
    w = f64(bf(w)).reshape(k // 32, 32, n)
    amax = np.abs(w).max(1)
    if fmt == "e4m3":
        byte = np.frexp(amax)[1] - 1 + 127 - 7
    else:
        mant, ex = np.frexp(amax / 6.0)
        byte = np.where(mant > 0.5, ex, ex - 1) + 127
    byte = np.clip(np.where(amax > 0, byte, 1), 1, 254)
    scaled = (w * np.exp2(127.0 - byte)[:, None, :]).reshape(k, n).astype(np.float32)
    by_word = np.ascontiguousarray(scaled.reshape(k // 512, 128, 4, n).transpose(0, 1, 3, 2))
    if fmt == "e4m3":
        words = by_word.astype(ml_dtypes.float8_e4m3fn).view(np.uint8)
    else:
        c = by_word.astype(ml_dtypes.float4_e2m1fn).view(np.uint8) & 0xF
        words = c[..., 0::2] | (c[..., 1::2] << 4)
    return np.ascontiguousarray(words), np.ascontiguousarray(byte.astype(np.uint8).reshape(k // 512, 16, n))


def unpack_weight(words, scales, fmt):
    g, p, n, _ = words.shape
    if fmt == "e4m3":
        vals = np.ascontiguousarray(words).view(ml_dtypes.float8_e4m3fn).astype(np.float64)
    else:
        nib = np.empty((g, p, n, 4), np.uint8)
        nib[..., 0::2] = words & 0xF
        nib[..., 1::2] = words >> 4
        vals = E2M1[nib]
    vals = vals * np.repeat(np.exp2(scales.astype(np.float64) - 127.0), 8, axis=1)[..., None]
    return vals.transpose(0, 1, 3, 2).reshape(g * 512, n)
def pack4(w):
    words, scales = pack_weight(w, "e2m1")
    return words.reshape(words.shape[0], 128, -1), scales


def unpack4(words, scales):
    return unpack_weight(words.reshape(words.shape[0], 128, -1, 2), scales, "e2m1")


def planes(Y):
    n, m = Y.shape
    b = f64(bf(Y)).reshape(n // 32, 32, m)
    amax = np.abs(b).max(1)
    byte = np.clip(np.where(amax > 0, np.frexp(amax)[1] - 1 + 127 - 7, 1), 1, 254)
    codes = (b * np.exp2(127.0 - byte)[:, None, :]).reshape(n, m).astype(np.float32).astype(ml_dtypes.float8_e4m3fn).view(np.uint8)
    words = codes.reshape(n // 512, 128, 4, m).transpose(0, 1, 3, 2)
    return np.ascontiguousarray(words), np.ascontiguousarray(byte.astype(np.uint8).reshape(n // 512, 16, m))


B, L, C = 8, 512, 512


def time_mixing(x, g_t, w_t, b_t):
    xt = x * g_t[None, :, None]
    m = (mxq(xt, 1, "e4m3").transpose(0, 2, 1) @ w_t).transpose(0, 2, 1) + b_t[None, :, None]
    return x + np.maximum(m, 0.0)


def feature_mixing(h, g_c, w_f, b_f):
    hg = h * g_c[None, None, :]
    q = (mxq(hg, 2, "e4m3") @ w_f) + b_f[None, None, :]
    return h + np.maximum(q, 0.0)


def setup_inputs():
    s, u = mx_kscale(L), mx_kscale(C)
    x = bf(np.random.standard_normal((B, L, C)))
    g_t = bf((1.0 + 0.1 * np.random.standard_normal(L)) * s)
    w_t_words, w_t_scales = pack4(np.random.standard_normal((L, L)) / np.sqrt(L) / s[:, None])
    b_t = bf(np.random.standard_normal(L) * 0.3)
    g_c = bf((1.0 + 0.1 * np.random.standard_normal(C)) * u)
    w_f_words, w_f_scales = pack4(np.random.standard_normal((C, C)) / np.sqrt(C) / u[:, None])
    b_f = bf(np.random.standard_normal(C) * 0.3)
    return {
        "x": x,
        "g_t": g_t,
        "w_t_words": w_t_words,
        "w_t_scales": w_t_scales,
        "b_t": b_t,
        "g_c": g_c,
        "w_f_words": w_f_words,
        "w_f_scales": w_f_scales,
        "b_f": b_f,
    }


def core(x, g_t, w_t_words, w_t_scales, b_t, g_c, w_f_words, w_f_scales, b_f):
    w_t = unpack4(w_t_words, w_t_scales)
    w_f = unpack4(w_f_words, w_f_scales)
    h = time_mixing(f64(x), f64(g_t), w_t, f64(b_t))
    return feature_mixing(h, f64(g_c), w_f, f64(b_f))


def reference(x, g_t, w_t_words, w_t_scales, b_t, g_c, w_f_words, w_f_scales, b_f):
    R_out = core(x, g_t, w_t_words, w_t_scales, b_t, g_c, w_f_words, w_f_scales, b_f)
    words, scales = planes(np.moveaxis(R_out, 2, 0).reshape(512, -1))
    return R_out, words, scales

@@ -1,0 +1,296 @@
+from contextlib import ExitStack
+
+import concourse.mybir as mybir
+from concourse.masks import make_identity
+
+F32 = mybir.dt.float32
+BF16 = mybir.dt.bfloat16
+I32 = mybir.dt.int32
+U32 = mybir.dt.uint32
+U8 = mybir.dt.uint8
+FP8X4 = mybir.dt.float8_e4m3fn_x4
+FP4X4 = mybir.dt.float4_e2m1fn_x4
+ALU = mybir.AluOpType
+ACT = mybir.ActivationFunctionType
+
+B, L, C = 8, 512, 512
+P = 128
+FLOPS = 2 * 2 * B * L * C * C
+
+
+def tile_tsmixertimethenfeaturemixing_x2_kernel(
+    tc, x, g_t, w_t_words, w_t_scales, b_t, g_c, w_f_words, w_f_scales, b_f, out, out_words, out_scales
+):
+    nc = tc.nc
+    with ExitStack() as ctx:
+        keep = ctx.enter_context(tc.tile_pool(name="keep", bufs=1))
+        work = ctx.enter_context(tc.tile_pool(name="work", bufs=2))
+        psum = ctx.enter_context(tc.psum_pool(name="psum", bufs=4))
+
+        gt = keep.tile([P, 4], BF16, name="gt")
+        gc = keep.tile([P, 4], BF16, name="gc")
+        rows = keep.tile([P, P], BF16, name="rows")
+        wt = keep.tile([P, 2 * L], U8, name="wt", align_bytes=64)
+        wf = keep.tile([P, 2 * C], U8, name="wf", align_bytes=64)
+        wts = keep.tile([P, L], U8, name="wts", align_bytes=64)
+        wfs = keep.tile([P, C], U8, name="wfs", align_bytes=64)
+        ident = keep.tile([P, P], F32, name="ident")
+        identb = keep.tile([P, P], BF16, name="identb")
+        bcol = keep.tile([P, 8], F32, name="bcol")
+        nbt = keep.tile([P, 4], F32, name="nbt")
+        gcf = keep.tile([P, 4], F32, name="gcf")
+        sc3 = keep.tile([P, B * L], U8, name="sc3", align_bytes=64)
+
+        nc.vector.memset(wts[:].bitcast(I32), 0)
+        nc.vector.memset(wfs[:].bitcast(I32), 0)
+        nc.vector.memset(rows[:], 0.0)
+        make_identity(nc, identb[:])
+        make_identity(nc, ident[:])
+
+        xa, xr = {}, {}
+
+        def load_x(b):
+            xa[b] = work.tile([P, 4, C], BF16, name="xa", bufs=4)
+            nc.sync.dma_start(out=xa[b][:], in_=x[b].rearrange("(p j) c -> p j c", j=4))
+
+        def load_res(b):
+            xr[b] = work.tile([P, 4, C], BF16, name="xr", bufs=4)
+            nc.sync.dma_start(out=xr[b][:], in_=x[b].rearrange("(i p) c -> p i c", p=P))
+
+        nc.scalar.dma_start(out=gt[:], in_=g_t.rearrange("(p j) -> p j", j=4))
+        load_x(0)
+        nc.sync.dma_start(out=wt[:].bitcast(I32), in_=w_t_words[0].bitcast(I32))
+        for q in range(4):
+            nc.scalar.dma_start(out=wts[32 * q : 32 * q + 4, :].bitcast(I32), in_=w_t_scales[0, 4 * q : 4 * q + 4, :].bitcast(I32))
+        nc.scalar.dma_start(out=rows[0:4, :], in_=b_t.rearrange("(i p) -> i p", p=P))
+        nc.scalar.dma_start(out=rows[4:8, :], in_=b_f.rearrange("(i p) -> i p", p=P))
+        nc.scalar.dma_start(out=gc[:], in_=g_c.rearrange("(p j) -> p j", j=4))
+        load_res(0)
+        nc.sync.dma_start(out=wf[:].bitcast(I32), in_=w_f_words[0].bitcast(I32))
+        for q in range(4):
+            nc.scalar.dma_start(out=wfs[32 * q : 32 * q + 4, :].bitcast(I32), in_=w_f_scales[0, 4 * q : 4 * q + 4, :].bitcast(I32))
+        load_x(1)
+        load_res(1)
+
+        xg, grouped, codes1, scale1 = {}, {}, {}, {}
+        h, xb, mt = {}, {}, {}
+        hgi, codes2, scale2, th = {}, {}, {}, {}
+        r2, qt, ot, ob, tr = {}, {}, {}, {}, {}
+        oi, wtp, codes3 = {}, {}, {}
+
+        def mult(b, part):
+            if part == 0:
+                xg[b] = work.tile([P, 4, C], BF16, name="xg", bufs=3, align_bytes=64)
+            for j in (2 * part, 2 * part + 1):
+                nc.vector.tensor_scalar_mul(out=xg[b][:, j, :], in0=xa[b][:, j, :], scalar1=gt[:, j : j + 1])
+
+        def interleave(b, half, eng):
+            if half == 0:
+                grouped[b] = work.tile([P, C, 4], BF16, name="grouped", align_bytes=64)
+            c = slice(half * 256, half * 256 + 256)
+            src = xg[b][:, :, c].rearrange("p j c -> p c j")
+            if eng == 0:
+                nc.scalar.copy(out=grouped[b][:, c, :], in_=src)
+            else:
+                nc.vector.tensor_copy(out=grouped[b][:, c, :], in_=src)
+
+        def quant1(b):
+            codes1[b] = work.tile([P, C], U32, name="codes1", align_bytes=64)
+            scale1[b] = work.tile([P, C], U8, name="scale1", align_bytes=64)
+            nc.vector.quantize_mx(out=codes1[b][:].bitcast(FP8X4), scales=scale1[b][:], in_=grouped[b][:].rearrange("p c j -> p (c j)"))
+
+        def mx1(u):
+            b, half = divmod(u, 2)
+            mt[u] = [None, None]
+            for k in (1, 0):
+                i = 2 * half + k
+                m = psum.tile([P, 512], F32, name="mx")
+                nc.tensor.matmul_mx(
+                    out=m[:],
+                    lhsT=wt[:, 256 * i : 256 * i + 256].bitcast(FP4X4),
+                    lhsT_scale=wts[:, P * i : P * i + P],
+                    rhs=codes1[b][:].bitcast(FP8X4),
+                    rhs_scale=scale1[b][:],
+                    start=True,
+                    stop=True,
+                )
+                mt[u][k] = m
+
+        def bias_res(u):
+            b, half = divmod(u, 2)
+            xb[u] = work.tile([P, 4, P], F32, name="xb", bufs=3)
+            i = 2 * half
+            nc.gpsimd.tensor_scalar(
+                out=xb[u][:], in0=xr[b][:, i, :].rearrange("p (c t) -> p t c", t=4), scalar1=1.0, scalar2=bcol[:, i : i + 1], op0=ALU.mult, op1=ALU.add
+            )
+
+        def relu_s(u):
+            b, half = divmod(u, 2)
+            h[u] = work.tile([P, 2, 4, P], F32, name="h", bufs=6)
+            i = 2 * half + 1
+            nc.scalar.activation(out=h[u][:, 1], in_=mt[u][1][:].rearrange("p (c t) -> p t c", t=4), func=ACT.Relu, bias=bcol[:, i : i + 1], scale=1.0)
+
+        def res_g(u):
+            b, half = divmod(u, 2)
+            i = 2 * half + 1
+            nc.gpsimd.tensor_tensor(out=h[u][:, 1], in0=h[u][:, 1], in1=xr[b][:, i, :].rearrange("p (c t) -> p t c", t=4), op=ALU.add)
+
+        def res_v(u):
+            b, half = divmod(u, 2)
+            i = 2 * half
+            nc.vector.scalar_tensor_tensor(
+                out=h[u][:, 0], in0=mt[u][0][:].rearrange("p (c t) -> p t c", t=4), scalar=nbt[:, i : i + 1], in1=xb[u][:], op0=ALU.max, op1=ALU.add
+            )
+
+        def trans_h(u):
+            th[u] = []
+            for k in range(2):
+                t_ = psum.tile([P, 4, P], F32, name="tp")
+                for t in range(4):
+                    nc.tensor.transpose(t_[:, t, :], h[u][:, k, t, :], ident[:])
+                th[u].append(t_)
+
+        def hg(u):
+            hgi[u] = work.tile([P, 2, P, 4], BF16, name="hgi", align_bytes=64)
+            for k in range(2):
+                nc.vector.tensor_tensor(
+                    out=hgi[u][:, k],
+                    in0=th[u][k][:].rearrange("p t s -> p s t"),
+                    in1=gcf[:].unsqueeze(1).to_broadcast([P, P, 4]),
+                    op=ALU.mult,
+                )
+
+        def quant2(u):
+            codes2[u] = work.tile([P, 256], U32, name="codes2", align_bytes=64)
+            scale2[u] = work.tile([P, 256], U8, name="scale2", align_bytes=64)
+            nc.vector.quantize_mx(out=codes2[u][:].bitcast(FP8X4), scales=scale2[u][:], in_=hgi[u][:].rearrange("p k s t -> p (k s t)"))
+
+        def mx2(u):
+            qt[u] = []
+            for d in range(2):
+                q = psum.tile([P, 2, 256], F32, name="mx")
+                for e in range(2):
+                    i = 2 * d + e
+                    nc.tensor.matmul_mx(
+                        out=q[:, e, :],
+                        lhsT=wf[:, 256 * i : 256 * i + 256].bitcast(FP4X4),
+                        lhsT_scale=wfs[:, P * i : P * i + P],
+                        rhs=codes2[u][:].bitcast(FP8X4),
+                        rhs_scale=scale2[u][:],
+                        start=True,
+                        stop=True,
+                    )
+                qt[u].append(q)
+
+        def relu2(u):
+            r2[u] = work.tile([P, 4, 256], F32, name="r2", bufs=3)
+            for i in range(4):
+                nc.scalar.activation(out=r2[u][:, i, :], in_=qt[u][i // 2][:, i % 2, :], func=ACT.Relu, bias=bcol[:, 4 + i : 5 + i], scale=1.0)
+
+        def trans_r(u):
+            tr[u] = []
+            for k in range(2):
+                t_ = psum.tile([P, 512], F32, name="tp")
+                for i in range(4):
+                    nc.tensor.transpose(t_[:, P * i : P * i + P], r2[u][:, i, P * k : P * k + P], ident[:])
+                tr[u].append(t_)
+
+        def outs(u):
+            b, half = divmod(u, 2)
+            ot[u] = work.tile([P, 2, C], F32, name="ot", bufs=4)
+            for k in range(2):
+                nc.vector.tensor_tensor(
+                    out=ot[u][:, k, :].rearrange("p (c t) -> p c t", t=4),
+                    in0=tr[u][k][:].rearrange("p (c t) -> p c t", t=4),
+                    in1=h[u][:, k].rearrange("p t c -> p c t"),
+                    op=ALU.add,
+                )
+            nc.sync.dma_start(out=out[b, 256 * half : 256 * half + 256, :].rearrange("(k p) c -> p k c", p=P), in_=ot[u][:])
+
+        def cast(u):
+            ob[u] = work.tile([P, 2, C], BF16, name="ob", bufs=3)
+            nc.gpsimd.tensor_scalar(out=ob[u][:], in0=ot[u][:], scalar1=1.0, scalar2=0.0, op0=ALU.mult, op1=ALU.add)
+
+        def trans_o(u):
+            wtp[u] = psum.tile([P, 2, 2, P], F32, name="tp")
+            for k in range(2):
+                words = ob[u][:, k, :].bitcast(F32)
+                for e in range(2):
+                    nc.tensor.transpose(wtp[u][:, k, e, :], words[:, e : 256 : 2], ident[:])
+
+        def pack_o(u):
+            b, half = divmod(u, 2)
+            if half == 0:
+                oi[b] = work.tile([P, L, 2], F32, name="oi", align_bytes=64)
+            nc.scalar.copy(
+                out=oi[b][:, 256 * half : 256 * half + 256, :].rearrange("p (k s) e -> p k s e", k=2), in_=wtp[u][:].rearrange("p k e s -> p k s e")
+            )
+
+        def quant3(b):
+            codes3[b] = work.tile([P, L], U32, name="codes3", bufs=3, align_bytes=64)
+            nc.vector.quantize_mx(
+                out=codes3[b][:].bitcast(FP8X4), scales=sc3[:, L * b : L * b + L], in_=oi[b][:].rearrange("p s e -> p (s e)").bitcast(BF16)
+            )
+            nc.sync.dma_start(out=out_words[0].rearrange("p m t -> p (m t)")[:, 4 * L * b : 4 * L * b + 4 * L].bitcast(I32), in_=codes3[b][:].bitcast(I32))
+
+        U = 2 * B
+        vt = psum.tile([P, P], BF16, name="tp")
+
+        with tc.manual_schedule():
+            mult(0, 0)
+            mult(0, 1)
+            interleave(0, 0, 0)
+            interleave(0, 1, 1)
+            quant1(0)
+            nc.tensor.transpose(vt[:], rows[:], identb[:])
+            nc.vector.tensor_copy(out=bcol[:], in_=vt[:, 0:8])
+            nc.vector.tensor_scalar_mul(out=nbt[:], in0=bcol[:, 0:4], scalar1=-1.0)
+            nc.vector.tensor_copy(out=gcf[:], in_=gc[:])
+            bias_res(0)
+            mult(1, 0)
+            mult(1, 1)
+            for n in range(U + 4):
+                b, half = divmod(n, 2)
+                if half == 0 and b + 2 < B:
+                    load_x(b + 2)
+                    load_res(b + 2)
+                if n < U:
+                    mx1(n)
+                if 0 <= n - 2 < U:
+                    trans_r(n - 2)
+                if 0 <= n - 3 < U:
+                    trans_o(n - 3)
+                if 0 <= n - 1 < U:
+                    hg(n - 1)
+                if half == 0 and n >= 5:
+                    quant3((n - 5) // 2)
+                if half == 1 and b + 2 < B:
+                    mult(b + 2, 1)
+                if n < U:
+                    relu_s(n)
+                if 0 <= n - 3 < U:
+                    pack_o(n - 3)
+                if n + 1 < U:
+                    bias_res(n + 1)
+                if 0 <= n - 1 < U:
+                    quant2(n - 1)
+                    mx2(n - 1)
+                if n < U:
+                    res_g(n)
+                    res_v(n)
+                if 0 <= n - 2 < U:
+                    outs(n - 2)
+                    cast(n - 2)
+                if b + 1 < B and n < U:
+                    interleave(b + 1, half, 0)
+                if 0 <= n - 1 < U:
+                    relu2(n - 1)
+                if n < U:
+                    trans_h(n)
+                if half == 0 and b + 2 < B:
+                    mult(b + 2, 0)
+                if half == 1 and b + 1 < B:
+                    quant1(b + 1)
+            quant3(B - 1)
+        for q in range(4):
+            nc.sync.dma_start(out=out_scales[0, 4 * q : 4 * q + 4, :].bitcast(I32), in_=sc3[32 * q : 32 * q + 4, :].bitcast(I32))

@@ -38,20 +38,25 @@ def tile_tsmixertimethenfeaturemixing_x2_kernel(
         identb = keep.tile([P, P], BF16, name="identb")
         bcol = keep.tile([P, 8], F32, name="bcol")
         nbt = keep.tile([P, 4], F32, name="nbt")
-        gcf = keep.tile([P, 4], F32, name="gcf")
         sc3 = keep.tile([P, B * L], U8, name="sc3", align_bytes=64)
 
-        nc.vector.memset(wts[:].bitcast(I32), 0)
-        nc.vector.memset(wfs[:].bitcast(I32), 0)
+        nc.gpsimd.memset(wts[:].bitcast(I32), 0)
         nc.vector.memset(rows[:], 0.0)
+        nc.vector.memset(wfs[:].bitcast(I32), 0)
         make_identity(nc, identb[:])
         make_identity(nc, ident[:])
 
         xa, xr = {}, {}
 
         def load_x(b):
-            xa[b] = work.tile([P, 4, C], BF16, name="xa", bufs=4)
-            nc.sync.dma_start(out=xa[b][:], in_=x[b].rearrange("(p j) c -> p j c", j=4))
+            if b == 0:
+                for part in range(2):
+                    xa[0, part] = work.tile([P, 4, C // 2], BF16, name="xa0", bufs=2)
+                    c = slice(part * C // 2, (part + 1) * C // 2)
+                    nc.sync.dma_start(out=xa[0, part][:], in_=x[0, :, c].rearrange("(p j) c -> p j c", j=4))
+            else:
+                xa[b] = work.tile([P, 4, C], BF16, name="xa", bufs=4)
+                nc.sync.dma_start(out=xa[b][:], in_=x[b].rearrange("(p j) c -> p j c", j=4))
 
         def load_res(b):
             xr[b] = work.tile([P, 4, C], BF16, name="xr", bufs=4)
@@ -59,19 +64,20 @@ def tile_tsmixertimethenfeaturemixing_x2_kernel(
 
         nc.scalar.dma_start(out=gt[:], in_=g_t.rearrange("(p j) -> p j", j=4))
         load_x(0)
-        nc.sync.dma_start(out=wt[:].bitcast(I32), in_=w_t_words[0].bitcast(I32))
-        for q in range(4):
-            nc.scalar.dma_start(out=wts[32 * q : 32 * q + 4, :].bitcast(I32), in_=w_t_scales[0, 4 * q : 4 * q + 4, :].bitcast(I32))
         nc.scalar.dma_start(out=rows[0:4, :], in_=b_t.rearrange("(i p) -> i p", p=P))
         nc.scalar.dma_start(out=rows[4:8, :], in_=b_f.rearrange("(i p) -> i p", p=P))
-        nc.scalar.dma_start(out=gc[:], in_=g_c.rearrange("(p j) -> p j", j=4))
+        for q in range(4):
+            nc.scalar.dma_start(out=wts[32 * q : 32 * q + 4, :].bitcast(I32), in_=w_t_scales[0, 4 * q : 4 * q + 4, :].bitcast(I32))
+        nc.sync.dma_start(out=wt[:].bitcast(I32), in_=w_t_words[0].bitcast(I32))
         load_res(0)
+        nc.scalar.dma_start(out=gc[:], in_=g_c.rearrange("(p j) -> p j", j=4))
+        load_x(1)
         nc.sync.dma_start(out=wf[:].bitcast(I32), in_=w_f_words[0].bitcast(I32))
         for q in range(4):
             nc.scalar.dma_start(out=wfs[32 * q : 32 * q + 4, :].bitcast(I32), in_=w_f_scales[0, 4 * q : 4 * q + 4, :].bitcast(I32))
-        load_x(1)
         load_res(1)
 
+        U = 2 * B
         xg, grouped, codes1, scale1 = {}, {}, {}, {}
         h, xb, mt = {}, {}, {}
         hgi, codes2, scale2, th = {}, {}, {}, {}
@@ -79,86 +85,112 @@ def tile_tsmixertimethenfeaturemixing_x2_kernel(
         oi, wtp, codes3 = {}, {}, {}
 
         def mult(b, part):
-            if part == 0:
-                xg[b] = work.tile([P, 4, C], BF16, name="xg", bufs=3, align_bytes=64)
-            for j in (2 * part, 2 * part + 1):
-                nc.vector.tensor_scalar_mul(out=xg[b][:, j, :], in0=xa[b][:, j, :], scalar1=gt[:, j : j + 1])
-
-        def interleave(b, half, eng):
-            if half == 0:
-                grouped[b] = work.tile([P, C, 4], BF16, name="grouped", align_bytes=64)
-            c = slice(half * 256, half * 256 + 256)
-            src = xg[b][:, :, c].rearrange("p j c -> p c j")
-            if eng == 0:
-                nc.scalar.copy(out=grouped[b][:, c, :], in_=src)
+            if b == 0:
+                xg[0, part] = work.tile([P, 4, C // 2], BF16, name="xg0", bufs=2, align_bytes=64)
+                src, dst, js = xa[0, part], xg[0, part], (0, 1, 2, 3)
             else:
-                nc.vector.tensor_copy(out=grouped[b][:, c, :], in_=src)
+                if b not in xg:
+                    xg[b] = work.tile([P, 4, C], BF16, name="xg", bufs=3, align_bytes=64)
+                src, dst, js = xa[b], xg[b], (2 * part, 2 * part + 1)
+            for j in js:
+                nc.vector.tensor_scalar_mul(out=dst[:, j, :], in0=src[:, j, :], scalar1=gt[:, j : j + 1])
 
-        def quant1(b):
-            codes1[b] = work.tile([P, C], U32, name="codes1", align_bytes=64)
-            scale1[b] = work.tile([P, C], U8, name="scale1", align_bytes=64)
-            nc.vector.quantize_mx(out=codes1[b][:].bitcast(FP8X4), scales=scale1[b][:], in_=grouped[b][:].rearrange("p c j -> p (c j)"))
+        def interleave(b, c0, c1, on_scalar):
+            if b not in grouped:
+                grouped[b] = work.tile([P, C, 4], BF16, name="grouped", align_bytes=64)
+            if b == 0:
+                part, off = divmod(c0, C // 2)
+                src = xg[0, part][:, :, off : off + c1 - c0].rearrange("p j c -> p c j")
+            else:
+                src = xg[b][:, :, c0:c1].rearrange("p j c -> p c j")
+            if on_scalar:
+                nc.scalar.copy(out=grouped[b][:, c0:c1, :], in_=src)
+            else:
+                nc.vector.tensor_copy(out=grouped[b][:, c0:c1, :], in_=src)
+
+        def quant1(b, c0=0, c1=C):
+            if c0 == 0:
+                codes1[b] = work.tile([P, C], U32, name="codes1", align_bytes=64)
+                scale1[b] = work.tile([P, C], U8, name="scale1", align_bytes=64)
+            nc.vector.quantize_mx(
+                out=codes1[b][:, c0:c1].bitcast(FP8X4), scales=scale1[b][:, c0:c1], in_=grouped[b][:, c0:c1, :].rearrange("p c j -> p (c j)")
+            )
+
+        def on_s(u, k):
+            return k == 1
 
         def mx1(u):
             b, half = divmod(u, 2)
-            mt[u] = [None, None]
-            for k in (1, 0):
-                i = 2 * half + k
-                m = psum.tile([P, 512], F32, name="mx")
-                nc.tensor.matmul_mx(
-                    out=m[:],
-                    lhsT=wt[:, 256 * i : 256 * i + 256].bitcast(FP4X4),
-                    lhsT_scale=wts[:, P * i : P * i + P],
-                    rhs=codes1[b][:].bitcast(FP8X4),
-                    rhs_scale=scale1[b][:],
-                    start=True,
-                    stop=True,
-                )
-                mt[u][k] = m
+            mt[u] = {k: psum.tile([P, 512], F32, name="mx") for k in (1, 0)}
+            step = 256 if u == 0 else C
+            for c0 in range(0, C, step):
+                for k in (1, 0):
+                    i = 2 * half + k
+                    for rep in range(1):
+                        nc.tensor.matmul_mx(
+                            out=mt[u][k][:, c0 : c0 + step],
+                            lhsT=wt[:, 256 * i : 256 * i + 256].bitcast(FP4X4),
+                            lhsT_scale=wts[:, P * i : P * i + P],
+                            rhs=codes1[b][:, c0 : c0 + step].bitcast(FP8X4),
+                            rhs_scale=scale1[b][:, c0 : c0 + step],
+                            start=True,
+                            stop=True,
+                        )
+
+        def perm(ap):
+            return ap.rearrange("p (c t) -> p t c", t=4)
 
         def bias_res(u):
             b, half = divmod(u, 2)
-            xb[u] = work.tile([P, 4, P], F32, name="xb", bufs=3)
-            i = 2 * half
-            nc.gpsimd.tensor_scalar(
-                out=xb[u][:], in0=xr[b][:, i, :].rearrange("p (c t) -> p t c", t=4), scalar1=1.0, scalar2=bcol[:, i : i + 1], op0=ALU.mult, op1=ALU.add
-            )
+            for k in (0, 1):
+                if not on_s(u, k):
+                    i = 2 * half + k
+                    xb[u, k] = work.tile([P, 4, P], F32, name="xb", bufs=3)
+                    if True:
+                        nc.scalar.activation(out=xb[u, k][:], in_=perm(xr[b][:, i, :]), func=ACT.Identity, bias=bcol[:, i : i + 1], scale=1.0)
+                    else:
+                        nc.gpsimd.tensor_scalar(
+                            out=xb[u, k][:], in0=perm(xr[b][:, i, :]), scalar1=1.0, scalar2=bcol[:, i : i + 1], op0=ALU.mult, op1=ALU.add
+                        )
 
         def relu_s(u):
             b, half = divmod(u, 2)
             h[u] = work.tile([P, 2, 4, P], F32, name="h", bufs=6)
-            i = 2 * half + 1
-            nc.scalar.activation(out=h[u][:, 1], in_=mt[u][1][:].rearrange("p (c t) -> p t c", t=4), func=ACT.Relu, bias=bcol[:, i : i + 1], scale=1.0)
+            for k in (1, 0):
+                if on_s(u, k):
+                    i = 2 * half + k
+                    nc.scalar.activation(out=h[u][:, k], in_=perm(mt[u][k][:]), func=ACT.Relu, bias=bcol[:, i : i + 1], scale=1.0)
 
         def res_g(u):
             b, half = divmod(u, 2)
-            i = 2 * half + 1
-            nc.gpsimd.tensor_tensor(out=h[u][:, 1], in0=h[u][:, 1], in1=xr[b][:, i, :].rearrange("p (c t) -> p t c", t=4), op=ALU.add)
+            for k in (1, 0):
+                if on_s(u, k):
+                    i = 2 * half + k
+                    nc.gpsimd.tensor_tensor(out=h[u][:, k], in0=h[u][:, k], in1=perm(xr[b][:, i, :]), op=ALU.add)
 
         def res_v(u):
             b, half = divmod(u, 2)
-            i = 2 * half
-            nc.vector.scalar_tensor_tensor(
-                out=h[u][:, 0], in0=mt[u][0][:].rearrange("p (c t) -> p t c", t=4), scalar=nbt[:, i : i + 1], in1=xb[u][:], op0=ALU.max, op1=ALU.add
+            for k in (0, 1):
+                if not on_s(u, k):
+                    i = 2 * half + k
+                    nc.vector.scalar_tensor_tensor(
+                        out=h[u][:, k], in0=perm(mt[u][k][:]), scalar=nbt[:, i : i + 1], in1=xb[u, k][:], op0=ALU.max, op1=ALU.add
+                    )
+
+        def trans_h(u, k):
+            th[u, k] = psum.tile([P, 4, P], F32, name="tp")
+            for t in range(4):
+                nc.tensor.transpose(th[u, k][:, t, :], h[u][:, k, t, :], ident[:])
+
+        def hg(u, k):
+            if u not in hgi:
+                hgi[u] = work.tile([P, 2, P, 4], BF16, name="hgi", align_bytes=64)
+            nc.vector.tensor_tensor(
+                out=hgi[u][:, k],
+                in0=th[u, k][:].rearrange("p t s -> p s t"),
+                in1=gc[:].unsqueeze(1).to_broadcast([P, P, 4]),
+                op=ALU.mult,
             )
-
-        def trans_h(u):
-            th[u] = []
-            for k in range(2):
-                t_ = psum.tile([P, 4, P], F32, name="tp")
-                for t in range(4):
-                    nc.tensor.transpose(t_[:, t, :], h[u][:, k, t, :], ident[:])
-                th[u].append(t_)
-
-        def hg(u):
-            hgi[u] = work.tile([P, 2, P, 4], BF16, name="hgi", align_bytes=64)
-            for k in range(2):
-                nc.vector.tensor_tensor(
-                    out=hgi[u][:, k],
-                    in0=th[u][k][:].rearrange("p t s -> p s t"),
-                    in1=gcf[:].unsqueeze(1).to_broadcast([P, P, 4]),
-                    op=ALU.mult,
-                )
 
         def quant2(u):
             codes2[u] = work.tile([P, 256], U32, name="codes2", align_bytes=64)
@@ -182,115 +214,215 @@ def tile_tsmixertimethenfeaturemixing_x2_kernel(
                     )
                 qt[u].append(q)
 
-        def relu2(u):
+        def relu2(u, engs="SSSS"):
             r2[u] = work.tile([P, 4, 256], F32, name="r2", bufs=3)
             for i in range(4):
-                nc.scalar.activation(out=r2[u][:, i, :], in_=qt[u][i // 2][:, i % 2, :], func=ACT.Relu, bias=bcol[:, 4 + i : 5 + i], scale=1.0)
+                src = qt[u][i // 2][:, i % 2, :]
+                if engs[i] == "S":
+                    nc.scalar.activation(out=r2[u][:, i, :], in_=src, func=ACT.Relu, bias=bcol[:, 4 + i : 5 + i], scale=1.0)
+                else:
+                    nc.vector.tensor_scalar(out=r2[u][:, i, :], in0=src, scalar1=bcol[:, 4 + i : 5 + i], scalar2=0.0, op0=ALU.add, op1=ALU.max)
 
-        def trans_r(u):
-            tr[u] = []
-            for k in range(2):
-                t_ = psum.tile([P, 512], F32, name="tp")
-                for i in range(4):
-                    nc.tensor.transpose(t_[:, P * i : P * i + P], r2[u][:, i, P * k : P * k + P], ident[:])
-                tr[u].append(t_)
+        def trans_r(u, k):
+            tr[u, k] = psum.tile([P, 512], F32, name="tp")
+            for i in range(4):
+                nc.tensor.transpose(tr[u, k][:, P * i : P * i + P], r2[u][:, i, P * k : P * k + P], ident[:])
 
-        def outs(u):
+        def outs(u, k):
             b, half = divmod(u, 2)
-            ot[u] = work.tile([P, 2, C], F32, name="ot", bufs=4)
-            for k in range(2):
-                nc.vector.tensor_tensor(
-                    out=ot[u][:, k, :].rearrange("p (c t) -> p c t", t=4),
-                    in0=tr[u][k][:].rearrange("p (c t) -> p c t", t=4),
-                    in1=h[u][:, k].rearrange("p t c -> p c t"),
-                    op=ALU.add,
-                )
-            nc.sync.dma_start(out=out[b, 256 * half : 256 * half + 256, :].rearrange("(k p) c -> p k c", p=P), in_=ot[u][:])
+            if u not in ot:
+                ot[u] = work.tile([P, 2, C], F32, name="ot", bufs=4)
+            nc.vector.tensor_tensor(
+                out=ot[u][:, k, :].rearrange("p (c t) -> p c t", t=4),
+                in0=tr[u, k][:].rearrange("p (c t) -> p c t", t=4),
+                in1=h[u][:, k].rearrange("p t c -> p c t"),
+                op=ALU.add,
+            )
+            if k == 1:
+                nc.sync.dma_start(out=out[b, 256 * half : 256 * half + 256, :].rearrange("(k p) c -> p k c", p=P), in_=ot[u][:])
 
-        def cast(u):
-            ob[u] = work.tile([P, 2, C], BF16, name="ob", bufs=3)
-            nc.gpsimd.tensor_scalar(out=ob[u][:], in0=ot[u][:], scalar1=1.0, scalar2=0.0, op0=ALU.mult, op1=ALU.add)
+        def cast(u, k, on_vector=False):
+            if u not in ob:
+                ob[u] = work.tile([P, 2, C], BF16, name="ob", bufs=3)
+            if on_vector:
+                nc.vector.tensor_copy(out=ob[u][:, k, :], in_=ot[u][:, k, :])
+            else:
+                nc.gpsimd.tensor_scalar(out=ob[u][:, k, :], in0=ot[u][:, k, :], scalar1=1.0, scalar2=0.0, op0=ALU.mult, op1=ALU.add)
 
-        def trans_o(u):
-            wtp[u] = psum.tile([P, 2, 2, P], F32, name="tp")
-            for k in range(2):
-                words = ob[u][:, k, :].bitcast(F32)
-                for e in range(2):
-                    nc.tensor.transpose(wtp[u][:, k, e, :], words[:, e : 256 : 2], ident[:])
+        def trans_o(u, k):
+            if u == U - 1:
+                wtp[u, k] = psum.tile([P, 1, 2, P], F32, name="tp")
+            elif (u, 0) not in wtp:
+                wtp[u, 0] = psum.tile([P, 2, 2, P], F32, name="tp")
+            dst = wtp[u, k][:, 0] if u == U - 1 else wtp[u, 0][:, k]
+            words = ob[u][:, k, :].bitcast(F32)
+            for e in range(2):
+                nc.tensor.transpose(dst[:, e, :], words[:, e : 256 : 2], ident[:])
 
         def pack_o(u):
             b, half = divmod(u, 2)
             if half == 0:
                 oi[b] = work.tile([P, L, 2], F32, name="oi", align_bytes=64)
-            nc.scalar.copy(
-                out=oi[b][:, 256 * half : 256 * half + 256, :].rearrange("p (k s) e -> p k s e", k=2), in_=wtp[u][:].rearrange("p k e s -> p k s e")
-            )
+            n = 1 if u == U - 1 else 2
+            for k in range(0, 2, n):
+                s0 = 256 * half + P * k
+                nc.scalar.copy(
+                    out=oi[b][:, s0 : s0 + P * n, :].rearrange("p (k s) e -> p k s e", k=n), in_=wtp[u, k][:].rearrange("p k e s -> p k s e")
+                )
 
-        def quant3(b):
-            codes3[b] = work.tile([P, L], U32, name="codes3", bufs=3, align_bytes=64)
+        def quant3(b, m0, m1):
+            if m0 == 0:
+                codes3[b] = work.tile([P, L], U32, name="codes3", bufs=3, align_bytes=64)
             nc.vector.quantize_mx(
-                out=codes3[b][:].bitcast(FP8X4), scales=sc3[:, L * b : L * b + L], in_=oi[b][:].rearrange("p s e -> p (s e)").bitcast(BF16)
+                out=codes3[b][:, m0:m1].bitcast(FP8X4),
+                scales=sc3[:, L * b + m0 : L * b + m1],
+                in_=oi[b][:, m0:m1, :].rearrange("p s e -> p (s e)").bitcast(BF16),
             )
-            nc.sync.dma_start(out=out_words[0].rearrange("p m t -> p (m t)")[:, 4 * L * b : 4 * L * b + 4 * L].bitcast(I32), in_=codes3[b][:].bitcast(I32))
+            w0 = 4 * L * b
+            nc.sync.dma_start(
+                out=out_words[0].rearrange("p m t -> p (m t)")[:, w0 + 4 * m0 : w0 + 4 * m1].bitcast(I32), in_=codes3[b][:, m0:m1].bitcast(I32)
+            )
 
-        U = 2 * B
+        def store_scales(b0, b1):
+            for q in range(4):
+                nc.scalar.dma_start(
+                    out=out_scales[0, 4 * q : 4 * q + 4, L * b0 : L * b1].bitcast(I32), in_=sc3[32 * q : 32 * q + 4, L * b0 : L * b1].bitcast(I32)
+                )
+
+        def quantize_result(b, part):
+            if 0 <= b < B - 1 and part == 0:
+                quant3(b, 0, 512)
+            elif b == B - 1:
+                quant3(b, 256 * part, 256 * part + 256)
+
         vt = psum.tile([P, P], BF16, name="tp")
 
         with tc.manual_schedule():
             mult(0, 0)
-            mult(0, 1)
-            interleave(0, 0, 0)
-            interleave(0, 1, 1)
-            quant1(0)
+            interleave(0, 0, 96, True)
+            interleave(0, 96, 256, False)
             nc.tensor.transpose(vt[:], rows[:], identb[:])
             nc.vector.tensor_copy(out=bcol[:], in_=vt[:, 0:8])
+            mult(0, 1)
+            interleave(0, 256, 352, True)
             nc.vector.tensor_scalar_mul(out=nbt[:], in0=bcol[:, 0:4], scalar1=-1.0)
-            nc.vector.tensor_copy(out=gcf[:], in_=gc[:])
+            interleave(0, 352, 512, False)
+            quant1(0, 0, 256)
+            quant1(0, 256, 512)
             bias_res(0)
+            mx1(0)
+            relu_s(0)
+            res_v(0)
+            bias_res(1)
+            res_g(0)
+            mx1(1)
+            relu_s(1)
+            res_v(1)
+            res_g(1)
             mult(1, 0)
             mult(1, 1)
-            for n in range(U + 4):
-                b, half = divmod(n, 2)
-                if half == 0 and b + 2 < B:
-                    load_x(b + 2)
-                    load_res(b + 2)
-                if n < U:
-                    mx1(n)
-                if 0 <= n - 2 < U:
-                    trans_r(n - 2)
-                if 0 <= n - 3 < U:
-                    trans_o(n - 3)
-                if 0 <= n - 1 < U:
-                    hg(n - 1)
-                if half == 0 and n >= 5:
-                    quant3((n - 5) // 2)
-                if half == 1 and b + 2 < B:
-                    mult(b + 2, 1)
-                if n < U:
-                    relu_s(n)
-                if 0 <= n - 3 < U:
-                    pack_o(n - 3)
-                if n + 1 < U:
-                    bias_res(n + 1)
-                if 0 <= n - 1 < U:
-                    quant2(n - 1)
-                    mx2(n - 1)
-                if n < U:
-                    res_g(n)
-                    res_v(n)
-                if 0 <= n - 2 < U:
-                    outs(n - 2)
-                    cast(n - 2)
-                if b + 1 < B and n < U:
-                    interleave(b + 1, half, 0)
-                if 0 <= n - 1 < U:
-                    relu2(n - 1)
-                if n < U:
-                    trans_h(n)
-                if half == 0 and b + 2 < B:
-                    mult(b + 2, 0)
-                if half == 1 and b + 1 < B:
-                    quant1(b + 1)
-            quant3(B - 1)
-        for q in range(4):
-            nc.sync.dma_start(out=out_scales[0, 4 * q : 4 * q + 4, :].bitcast(I32), in_=sc3[32 * q : 32 * q + 4, :].bitcast(I32))
+            load_x(2)
+            trans_h(0, 0)
+            trans_h(0, 1)
+            for r in range(-1, B + 3):
+                if 1 <= r + 1 < B:
+                    interleave(r + 1, 0, 256, True)
+                if 0 <= 2 * r - 4 < U:
+                    trans_o(2 * r - 4, 0)
+                if 0 <= 2 * r - 2 < U:
+                    mx2(2 * r - 2)
+                if 0 <= 2 * r - 2 < U:
+                    relu2(2 * r - 2)
+                if 2 <= 2 * r < U:
+                    bias_res(2 * r)
+                if 0 <= 2 * r - 4 < U:
+                    pack_o(2 * r - 4)
+                if 3 <= r + 3 < B:
+                    load_x(r + 3)
+                if 2 <= r + 1 < B:
+                    load_res(r + 1)
+                if 2 <= 2 * r - 1 < U:
+                    res_g(2 * r - 1)
+                if 0 <= 2 * r - 3 < U:
+                    outs(2 * r - 3, 0)
+                if 1 <= r < B:
+                    quant1(r)
+                if 0 <= 2 * r - 3 < U:
+                    cast(2 * r - 3, 0, 2 * r - 3 >= U - 2)
+                if 2 <= 2 * r + 1 < U:
+                    bias_res(2 * r + 1)
+                if 0 <= 2 * r - 3 < U:
+                    outs(2 * r - 3, 1)
+                if 1 <= 2 * r - 1 < U:
+                    trans_h(2 * r - 1, 1)
+                if 1 <= 2 * r - 1 < U:
+                    trans_h(2 * r - 1, 0)
+                if 0 <= 2 * r - 3 < U:
+                    cast(2 * r - 3, 1, 2 * r - 3 >= U - 2)
+                if 2 <= 2 * r < U:
+                    mx1(2 * r)
+                if 0 <= 2 * r - 1 < U:
+                    hg(2 * r - 1, 1)
+                if 0 <= 2 * r - 2 < U:
+                    trans_r(2 * r - 2, 0)
+                if 2 <= 2 * r < U:
+                    relu_s(2 * r)
+                if 0 <= 2 * r - 1 < U:
+                    hg(2 * r - 1, 0)
+                if 2 <= 2 * r < U:
+                    res_g(2 * r)
+                if 0 <= 2 * r - 3 < U:
+                    trans_o(2 * r - 3, 1)
+                if 2 <= r + 2 < B:
+                    mult(r + 2, 1)
+                if 0 <= 2 * r - 2 < U:
+                    trans_r(2 * r - 2, 1)
+                if 0 <= 2 * r - 1 < U:
+                    quant2(2 * r - 1)
+                if 2 <= r + 2 < B:
+                    mult(r + 2, 0)
+                if 0 <= 2 * r - 3 < U:
+                    trans_o(2 * r - 3, 0)
+                if 0 <= 2 * r - 1 < U:
+                    mx2(2 * r - 1)
+                if 2 <= 2 * r < U:
+                    res_v(2 * r)
+                quantize_result(r - 3, 1)
+                if 0 <= 2 * r - 3 < U:
+                    pack_o(2 * r - 3)
+                if 0 <= 2 * r - 2 < U:
+                    outs(2 * r - 2, 0)
+                if 0 <= 2 * r - 1 < U:
+                    relu2(2 * r - 1)
+                if 1 <= r + 1 < B:
+                    interleave(r + 1, 256, 512, True)
+                if 0 <= 2 * r - 2 < U:
+                    outs(2 * r - 2, 1)
+                if 0 <= 2 * r - 2 < U:
+                    cast(2 * r - 2, 1, 2 * r - 2 >= U - 2)
+                if 1 <= 2 * r < U:
+                    trans_h(2 * r, 0)
+                if 1 <= 2 * r < U:
+                    trans_h(2 * r, 1)
+                quantize_result(r - 2, 0)
+                if 0 <= 2 * r < U:
+                    hg(2 * r, 1)
+                if 0 <= 2 * r - 1 < U:
+                    trans_r(2 * r - 1, 0)
+                if 2 <= 2 * r + 1 < U:
+                    mx1(2 * r + 1)
+                if 0 <= 2 * r - 1 < U:
+                    trans_r(2 * r - 1, 1)
+                if 0 <= 2 * r < U:
+                    hg(2 * r, 0)
+                if 0 <= 2 * r < U:
+                    quant2(2 * r)
+                if 0 <= 2 * r - 2 < U:
+                    trans_o(2 * r - 2, 1)
+                if 0 <= 2 * r - 2 < U:
+                    cast(2 * r - 2, 0, 2 * r - 2 >= U - 2)
+                if 2 <= 2 * r + 1 < U:
+                    relu_s(2 * r + 1)
+                if 2 <= 2 * r + 1 < U:
+                    res_v(2 * r + 1)
+            store_scales(0, B)

@@ -116,8 +116,11 @@ def tile_tsmixertimethenfeaturemixing_x2_kernel(
                 out=codes1[b][:, c0:c1].bitcast(FP8X4), scales=scale1[b][:, c0:c1], in_=grouped[b][:, c0:c1, :].rearrange("p c j -> p (c j)")
             )
 
+        def on_p(u, k):
+            return False
+
         def on_s(u, k):
-            return k == 1
+            return on_p(u, k) or k == 1
 
         def mx1(u):
             b, half = divmod(u, 2)
@@ -126,7 +129,7 @@ def tile_tsmixertimethenfeaturemixing_x2_kernel(
             for c0 in range(0, C, step):
                 for k in (1, 0):
                     i = 2 * half + k
-                    for rep in range(1):
+                    for rep in range(2 if True else 1):
                         nc.tensor.matmul_mx(
                             out=mt[u][k][:, c0 : c0 + step],
                             lhsT=wt[:, 256 * i : 256 * i + 256].bitcast(FP4X4),
@@ -164,7 +167,7 @@ def tile_tsmixertimethenfeaturemixing_x2_kernel(
         def res_g(u):
             b, half = divmod(u, 2)
             for k in (1, 0):
-                if on_s(u, k):
+                if on_s(u, k) and not on_p(u, k):
                     i = 2 * half + k
                     nc.gpsimd.tensor_tensor(out=h[u][:, k], in0=h[u][:, k], in1=perm(xr[b][:, i, :]), op=ALU.add)
 
@@ -179,8 +182,15 @@ def tile_tsmixertimethenfeaturemixing_x2_kernel(
 
         def trans_h(u, k):
             th[u, k] = psum.tile([P, 4, P], F32, name="tp")
+            b, half = divmod(u, 2)
+            if on_p(u, k):
+                for t in range(4):
+                    nc.tensor.matmul(th[u, k][:, t, :], lhsT=xr[b][:, 2 * half + k, t:C:4], rhs=identb[:], start=t == 0, stop=False)
             for t in range(4):
-                nc.tensor.transpose(th[u, k][:, t, :], h[u][:, k, t, :], ident[:])
+                if on_p(u, k):
+                    nc.tensor.matmul(th[u, k][:, t, :], lhsT=h[u][:, k, t, :], rhs=ident[:], start=False, stop=t == 3, is_transpose=True)
+                else:
+                    nc.tensor.transpose(th[u, k][:, t, :], h[u][:, k, t, :], ident[:])
 
         def hg(u, k):
             if u not in hgi:
@@ -225,8 +235,15 @@ def tile_tsmixertimethenfeaturemixing_x2_kernel(
 
         def trans_r(u, k):
             tr[u, k] = psum.tile([P, 512], F32, name="tp")
+            b, half = divmod(u, 2)
+            if on_p(u, k):
+                nc.tensor.matmul(tr[u, k][:], lhsT=identb[:], rhs=xr[b][:, 2 * half + k, :], start=True, stop=False)
             for i in range(4):
-                nc.tensor.transpose(tr[u, k][:, P * i : P * i + P], r2[u][:, i, P * k : P * k + P], ident[:])
+                dst, src = tr[u, k][:, P * i : P * i + P], r2[u][:, i, P * k : P * k + P]
+                if on_p(u, k):
+                    nc.tensor.matmul(dst, lhsT=src, rhs=ident[:], start=False, stop=i == 3, is_transpose=True)
+                else:
+                    nc.tensor.transpose(dst, src, ident[:])
 
         def outs(u, k):
             b, half = divmod(u, 2)
@@ -244,10 +261,12 @@ def tile_tsmixertimethenfeaturemixing_x2_kernel(
         def cast(u, k, on_vector=False):
             if u not in ob:
                 ob[u] = work.tile([P, 2, C], BF16, name="ob", bufs=3)
+            dst = ob[u][:, k, :].rearrange("p (e c f) -> p e c f", e=2, f=2)
+            src = ot[u][:, k, :].rearrange("p (c e f) -> p e c f", e=2, f=2)
             if on_vector:
-                nc.vector.tensor_copy(out=ob[u][:, k, :], in_=ot[u][:, k, :])
+                nc.vector.tensor_copy(out=dst, in_=src)
             else:
-                nc.gpsimd.tensor_scalar(out=ob[u][:, k, :], in0=ot[u][:, k, :], scalar1=1.0, scalar2=0.0, op0=ALU.mult, op1=ALU.add)
+                nc.gpsimd.tensor_scalar(out=dst, in0=src, scalar1=1.0, scalar2=0.0, op0=ALU.mult, op1=ALU.add)
 
         def trans_o(u, k):
             if u == U - 1:
@@ -257,7 +276,7 @@ def tile_tsmixertimethenfeaturemixing_x2_kernel(
             dst = wtp[u, k][:, 0] if u == U - 1 else wtp[u, 0][:, k]
             words = ob[u][:, k, :].bitcast(F32)
             for e in range(2):
-                nc.tensor.transpose(dst[:, e, :], words[:, e : 256 : 2], ident[:])
+                nc.tensor.transpose(dst[:, e, :], words[:, P * e : P * e + P], ident[:])
 
         def pack_o(u):
             b, half = divmod(u, 2)
@@ -324,105 +343,105 @@ def tile_tsmixertimethenfeaturemixing_x2_kernel(
             load_x(2)
             trans_h(0, 0)
             trans_h(0, 1)
-            for r in range(-1, B + 3):
+            for r in range(-1, B + 4):
+                if 1 <= r < B:
+                    interleave(r, 256, 512, True)
+                if 0 <= 2 * r - 3 < U:
+                    relu2(2 * r - 3)
+                if 1 <= 2 * r - 2 < U:
+                    trans_h(2 * r - 2, 1)
+                if 0 <= 2 * r - 4 < U:
+                    outs(2 * r - 4, 0)
+                if 0 <= 2 * r - 5 < U:
+                    trans_o(2 * r - 5, 0)
+                if 2 <= r + 1 < B:
+                    load_res(r + 1)
+                if 2 <= r + 1 < B:
+                    mult(r + 1, 0)
+                if 0 <= 2 * r - 4 < U:
+                    outs(2 * r - 4, 1)
+                quantize_result(r - 4, 1)
+                if 0 <= 2 * r - 4 < U:
+                    cast(2 * r - 4, 1, 2 * r - 4 >= U - 2)
+                if 1 <= 2 * r - 2 < U:
+                    trans_h(2 * r - 2, 0)
+                if 3 <= r + 4 < B:
+                    load_x(r + 4)
+                if 0 <= 2 * r - 5 < U:
+                    pack_o(2 * r - 5)
+                if 0 <= 2 * r - 2 < U:
+                    hg(2 * r - 2, 1)
+                if 0 <= 2 * r - 2 < U:
+                    hg(2 * r - 2, 0)
+                quantize_result(r - 3, 0)
+                if 0 <= 2 * r - 3 < U:
+                    trans_r(2 * r - 3, 0)
+                if 2 <= 2 * r - 1 < U:
+                    mx1(2 * r - 1)
+                if 0 <= 2 * r - 2 < U:
+                    quant2(2 * r - 2)
+                if 0 <= 2 * r - 4 < U:
+                    trans_o(2 * r - 4, 1)
+                if 1 <= r < B:
+                    quant1(r)
                 if 1 <= r + 1 < B:
                     interleave(r + 1, 0, 256, True)
                 if 0 <= 2 * r - 4 < U:
-                    trans_o(2 * r - 4, 0)
+                    cast(2 * r - 4, 0, 2 * r - 4 >= U - 2)
+                if 2 <= 2 * r - 1 < U:
+                    relu_s(2 * r - 1)
                 if 0 <= 2 * r - 2 < U:
                     mx2(2 * r - 2)
-                if 0 <= 2 * r - 2 < U:
-                    relu2(2 * r - 2)
-                if 2 <= 2 * r < U:
-                    bias_res(2 * r)
-                if 0 <= 2 * r - 4 < U:
-                    pack_o(2 * r - 4)
-                if 3 <= r + 3 < B:
-                    load_x(r + 3)
-                if 2 <= r + 1 < B:
-                    load_res(r + 1)
+                if 2 <= 2 * r - 1 < U:
+                    res_v(2 * r - 1)
+                if 0 <= 2 * r - 3 < U:
+                    trans_r(2 * r - 3, 1)
+                if 1 <= 2 * r - 1 < U:
+                    trans_h(2 * r - 1, 0)
                 if 2 <= 2 * r - 1 < U:
                     res_g(2 * r - 1)
-                if 0 <= 2 * r - 3 < U:
-                    outs(2 * r - 3, 0)
-                if 1 <= r < B:
-                    quant1(r)
-                if 0 <= 2 * r - 3 < U:
-                    cast(2 * r - 3, 0, 2 * r - 3 >= U - 2)
                 if 2 <= 2 * r + 1 < U:
                     bias_res(2 * r + 1)
+                if 0 <= 2 * r - 3 < U:
+                    outs(2 * r - 3, 0)
+                if 0 <= 2 * r - 4 < U:
+                    trans_o(2 * r - 4, 0)
                 if 0 <= 2 * r - 3 < U:
                     outs(2 * r - 3, 1)
                 if 1 <= 2 * r - 1 < U:
                     trans_h(2 * r - 1, 1)
-                if 1 <= 2 * r - 1 < U:
-                    trans_h(2 * r - 1, 0)
+                if 0 <= 2 * r - 3 < U:
+                    cast(2 * r - 3, 0, 2 * r - 3 >= U - 2)
+                if 0 <= 2 * r - 2 < U:
+                    relu2(2 * r - 2)
+                if 0 <= 2 * r - 1 < U:
+                    hg(2 * r - 1, 0)
+                if 0 <= 2 * r - 1 < U:
+                    hg(2 * r - 1, 1)
+                if 2 <= r + 2 < B:
+                    mult(r + 2, 1)
                 if 0 <= 2 * r - 3 < U:
                     cast(2 * r - 3, 1, 2 * r - 3 >= U - 2)
                 if 2 <= 2 * r < U:
                     mx1(2 * r)
+                if 0 <= 2 * r - 4 < U:
+                    pack_o(2 * r - 4)
                 if 0 <= 2 * r - 1 < U:
-                    hg(2 * r - 1, 1)
+                    quant2(2 * r - 1)
+                if 2 <= 2 * r < U:
+                    bias_res(2 * r)
+                if 2 <= 2 * r < U:
+                    relu_s(2 * r)
                 if 0 <= 2 * r - 2 < U:
                     trans_r(2 * r - 2, 0)
                 if 2 <= 2 * r < U:
-                    relu_s(2 * r)
-                if 0 <= 2 * r - 1 < U:
-                    hg(2 * r - 1, 0)
+                    res_v(2 * r)
+                if 0 <= 2 * r - 2 < U:
+                    trans_r(2 * r - 2, 1)
                 if 2 <= 2 * r < U:
                     res_g(2 * r)
                 if 0 <= 2 * r - 3 < U:
                     trans_o(2 * r - 3, 1)
-                if 2 <= r + 2 < B:
-                    mult(r + 2, 1)
-                if 0 <= 2 * r - 2 < U:
-                    trans_r(2 * r - 2, 1)
-                if 0 <= 2 * r - 1 < U:
-                    quant2(2 * r - 1)
-                if 2 <= r + 2 < B:
-                    mult(r + 2, 0)
-                if 0 <= 2 * r - 3 < U:
-                    trans_o(2 * r - 3, 0)
                 if 0 <= 2 * r - 1 < U:
                     mx2(2 * r - 1)
-                if 2 <= 2 * r < U:
-                    res_v(2 * r)
-                quantize_result(r - 3, 1)
-                if 0 <= 2 * r - 3 < U:
-                    pack_o(2 * r - 3)
-                if 0 <= 2 * r - 2 < U:
-                    outs(2 * r - 2, 0)
-                if 0 <= 2 * r - 1 < U:
-                    relu2(2 * r - 1)
-                if 1 <= r + 1 < B:
-                    interleave(r + 1, 256, 512, True)
-                if 0 <= 2 * r - 2 < U:
-                    outs(2 * r - 2, 1)
-                if 0 <= 2 * r - 2 < U:
-                    cast(2 * r - 2, 1, 2 * r - 2 >= U - 2)
-                if 1 <= 2 * r < U:
-                    trans_h(2 * r, 0)
-                if 1 <= 2 * r < U:
-                    trans_h(2 * r, 1)
-                quantize_result(r - 2, 0)
-                if 0 <= 2 * r < U:
-                    hg(2 * r, 1)
-                if 0 <= 2 * r - 1 < U:
-                    trans_r(2 * r - 1, 0)
-                if 2 <= 2 * r + 1 < U:
-                    mx1(2 * r + 1)
-                if 0 <= 2 * r - 1 < U:
-                    trans_r(2 * r - 1, 1)
-                if 0 <= 2 * r < U:
-                    hg(2 * r, 0)
-                if 0 <= 2 * r < U:
-                    quant2(2 * r)
-                if 0 <= 2 * r - 2 < U:
-                    trans_o(2 * r - 2, 1)
-                if 0 <= 2 * r - 2 < U:
-                    cast(2 * r - 2, 0, 2 * r - 2 >= U - 2)
-                if 2 <= 2 * r + 1 < U:
-                    relu_s(2 * r + 1)
-                if 2 <= 2 * r + 1 < U:
-                    res_v(2 * r + 1)
             store_scales(0, B)

@@ -15,6 +15,7 @@ ACT = mybir.ActivationFunctionType
 
 B, L, C = 8, 512, 512
 P = 128
+U = 2 * B
 FLOPS = 2 * 2 * B * L * C * C
 
 
@@ -29,60 +30,42 @@ def tile_tsmixertimethenfeaturemixing_x2_kernel(
 
         gt = keep.tile([P, 4], BF16, name="gt")
         gc = keep.tile([P, 4], BF16, name="gc")
+        bt16 = keep.tile([P, 4], BF16, name="bt16")
         rows = keep.tile([P, P], BF16, name="rows")
+        wt_raw = keep.tile([P, 2 * L], U8, name="wt_raw", align_bytes=64)
+        wts_raw = keep.tile([P, L], U8, name="wts_raw", align_bytes=64)
         wt = keep.tile([P, 2 * L], U8, name="wt", align_bytes=64)
-        wf = keep.tile([P, 2 * C], U8, name="wf", align_bytes=64)
         wts = keep.tile([P, L], U8, name="wts", align_bytes=64)
+        wf = keep.tile([P, 2 * C], U8, name="wf", align_bytes=64)
         wfs = keep.tile([P, C], U8, name="wfs", align_bytes=64)
         ident = keep.tile([P, P], F32, name="ident")
         identb = keep.tile([P, P], BF16, name="identb")
-        bcol = keep.tile([P, 8], F32, name="bcol")
+        bt = keep.tile([P, 4], F32, name="bt")
         nbt = keep.tile([P, 4], F32, name="nbt")
+        bf = keep.tile([P, 4], F32, name="bf")
         sc3 = keep.tile([P, B * L], U8, name="sc3", align_bytes=64)
 
-        nc.gpsimd.memset(wts[:].bitcast(I32), 0)
-        nc.vector.memset(rows[:], 0.0)
-        nc.vector.memset(wfs[:].bitcast(I32), 0)
-        make_identity(nc, identb[:])
-        make_identity(nc, ident[:])
+        xa, xg, grouped, codes1, scale1 = {}, {}, {}, {}, {}
+        mt, h, xb, th, hgi, codes2, scale2 = {}, {}, {}, {}, {}, {}, {}
+        qt, r2, tr, ot, ob, wtp, oi, codes3 = {}, {}, {}, {}, {}, {}, {}, {}
 
-        xa, xr = {}, {}
+        def on_p(u, k):
+            return k == 1 and u % 4 != 3
+
+        def on_s(u, k):
+            return on_p(u, k) or k == 1 or u % 4 == 1
+
+        def perm(ap):
+            return ap.rearrange("p (c t) -> p t c", t=4)
+
+        def load_half(part):
+            xa[0, part] = work.tile([P, 4, C // 2], BF16, name="xa0", bufs=2)
+            c = slice(part * C // 2, (part + 1) * C // 2)
+            nc.sync.dma_start(out=xa[0, part][:], in_=x[0, :, c].rearrange("(p j) c -> p j c", j=4))
 
         def load_x(b):
-            if b == 0:
-                for part in range(2):
-                    xa[0, part] = work.tile([P, 4, C // 2], BF16, name="xa0", bufs=2)
-                    c = slice(part * C // 2, (part + 1) * C // 2)
-                    nc.sync.dma_start(out=xa[0, part][:], in_=x[0, :, c].rearrange("(p j) c -> p j c", j=4))
-            else:
-                xa[b] = work.tile([P, 4, C], BF16, name="xa", bufs=4)
-                nc.sync.dma_start(out=xa[b][:], in_=x[b].rearrange("(p j) c -> p j c", j=4))
-
-        def load_res(b):
-            xr[b] = work.tile([P, 4, C], BF16, name="xr", bufs=4)
-            nc.sync.dma_start(out=xr[b][:], in_=x[b].rearrange("(i p) c -> p i c", p=P))
-
-        nc.scalar.dma_start(out=gt[:], in_=g_t.rearrange("(p j) -> p j", j=4))
-        load_x(0)
-        nc.scalar.dma_start(out=rows[0:4, :], in_=b_t.rearrange("(i p) -> i p", p=P))
-        nc.scalar.dma_start(out=rows[4:8, :], in_=b_f.rearrange("(i p) -> i p", p=P))
-        for q in range(4):
-            nc.scalar.dma_start(out=wts[32 * q : 32 * q + 4, :].bitcast(I32), in_=w_t_scales[0, 4 * q : 4 * q + 4, :].bitcast(I32))
-        nc.sync.dma_start(out=wt[:].bitcast(I32), in_=w_t_words[0].bitcast(I32))
-        load_res(0)
-        nc.scalar.dma_start(out=gc[:], in_=g_c.rearrange("(p j) -> p j", j=4))
-        load_x(1)
-        nc.sync.dma_start(out=wf[:].bitcast(I32), in_=w_f_words[0].bitcast(I32))
-        for q in range(4):
-            nc.scalar.dma_start(out=wfs[32 * q : 32 * q + 4, :].bitcast(I32), in_=w_f_scales[0, 4 * q : 4 * q + 4, :].bitcast(I32))
-        load_res(1)
-
-        U = 2 * B
-        xg, grouped, codes1, scale1 = {}, {}, {}, {}
-        h, xb, mt = {}, {}, {}
-        hgi, codes2, scale2, th = {}, {}, {}, {}
-        r2, qt, ot, ob, tr = {}, {}, {}, {}, {}
-        oi, wtp, codes3 = {}, {}, {}
+            xa[b] = work.tile([P, 4, C], BF16, name="xa", bufs=7)
+            nc.sync.dma_start(out=xa[b][:], in_=x[b].rearrange("(p j) c -> p j c", j=4))
 
         def mult(b, part):
             if b == 0:
@@ -90,37 +73,34 @@ def tile_tsmixertimethenfeaturemixing_x2_kernel(
                 src, dst, js = xa[0, part], xg[0, part], (0, 1, 2, 3)
             else:
                 if b not in xg:
-                    xg[b] = work.tile([P, 4, C], BF16, name="xg", bufs=3, align_bytes=64)
+                    xg[b] = work.tile([P, 4, C], BF16, name="xg", bufs=4, align_bytes=64)
                 src, dst, js = xa[b], xg[b], (2 * part, 2 * part + 1)
             for j in js:
                 nc.vector.tensor_scalar_mul(out=dst[:, j, :], in0=src[:, j, :], scalar1=gt[:, j : j + 1])
 
-        def interleave(b, c0, c1, on_scalar):
+        def interleave(b, c0, c1, eng):
             if b not in grouped:
-                grouped[b] = work.tile([P, C, 4], BF16, name="grouped", align_bytes=64)
+                grouped[b] = work.tile([P, C, 4], BF16, name="grouped", bufs=4, align_bytes=64)
             if b == 0:
                 part, off = divmod(c0, C // 2)
                 src = xg[0, part][:, :, off : off + c1 - c0].rearrange("p j c -> p c j")
             else:
                 src = xg[b][:, :, c0:c1].rearrange("p j c -> p c j")
-            if on_scalar:
-                nc.scalar.copy(out=grouped[b][:, c0:c1, :], in_=src)
+            dst = grouped[b][:, c0:c1, :]
+            if eng == "S":
+                nc.scalar.copy(out=dst, in_=src)
+            elif eng == "G":
+                nc.gpsimd.tensor_scalar(out=dst, in0=src, scalar1=1.0, scalar2=0.0, op0=ALU.mult, op1=ALU.add)
             else:
-                nc.vector.tensor_copy(out=grouped[b][:, c0:c1, :], in_=src)
+                nc.vector.tensor_copy(out=dst, in_=src)
 
         def quant1(b, c0=0, c1=C):
-            if c0 == 0:
-                codes1[b] = work.tile([P, C], U32, name="codes1", align_bytes=64)
-                scale1[b] = work.tile([P, C], U8, name="scale1", align_bytes=64)
+            if b not in codes1:
+                codes1[b] = work.tile([P, C], U32, name="codes1", bufs=4, align_bytes=64)
+                scale1[b] = work.tile([P, C], U8, name="scale1", bufs=4, align_bytes=64)
             nc.vector.quantize_mx(
                 out=codes1[b][:, c0:c1].bitcast(FP8X4), scales=scale1[b][:, c0:c1], in_=grouped[b][:, c0:c1, :].rearrange("p c j -> p (c j)")
             )
-
-        def on_p(u, k):
-            return False
-
-        def on_s(u, k):
-            return on_p(u, k) or k == 1
 
         def mx1(u):
             b, half = divmod(u, 2)
@@ -128,32 +108,28 @@ def tile_tsmixertimethenfeaturemixing_x2_kernel(
             step = 256 if u == 0 else C
             for c0 in range(0, C, step):
                 for k in (1, 0):
-                    i = 2 * half + k
-                    for rep in range(2 if True else 1):
-                        nc.tensor.matmul_mx(
-                            out=mt[u][k][:, c0 : c0 + step],
-                            lhsT=wt[:, 256 * i : 256 * i + 256].bitcast(FP4X4),
-                            lhsT_scale=wts[:, P * i : P * i + P],
-                            rhs=codes1[b][:, c0 : c0 + step].bitcast(FP8X4),
-                            rhs_scale=scale1[b][:, c0 : c0 + step],
-                            start=True,
-                            stop=True,
-                        )
-
-        def perm(ap):
-            return ap.rearrange("p (c t) -> p t c", t=4)
+                    j = 2 * half + k
+                    nc.tensor.matmul_mx(
+                        out=mt[u][k][:, c0 : c0 + step],
+                        lhsT=wt[:, 256 * j : 256 * j + 256].bitcast(FP4X4),
+                        lhsT_scale=wts[:, P * j : P * j + P],
+                        rhs=codes1[b][:, c0 : c0 + step].bitcast(FP8X4),
+                        rhs_scale=scale1[b][:, c0 : c0 + step],
+                        start=True,
+                        stop=True,
+                    )
 
         def bias_res(u):
             b, half = divmod(u, 2)
             for k in (0, 1):
                 if not on_s(u, k):
-                    i = 2 * half + k
+                    j = 2 * half + k
                     xb[u, k] = work.tile([P, 4, P], F32, name="xb", bufs=3)
-                    if True:
-                        nc.scalar.activation(out=xb[u, k][:], in_=perm(xr[b][:, i, :]), func=ACT.Identity, bias=bcol[:, i : i + 1], scale=1.0)
+                    if False:
+                        nc.scalar.activation(out=xb[u, k][:], in_=perm(xa[b][:, j, :]), func=ACT.Identity, bias=bt[:, j : j + 1], scale=1.0)
                     else:
                         nc.gpsimd.tensor_scalar(
-                            out=xb[u, k][:], in0=perm(xr[b][:, i, :]), scalar1=1.0, scalar2=bcol[:, i : i + 1], op0=ALU.mult, op1=ALU.add
+                            out=xb[u, k][:], in0=perm(xa[b][:, j, :]), scalar1=1.0, scalar2=bt[:, j : j + 1], op0=ALU.mult, op1=ALU.add
                         )
 
         def relu_s(u):
@@ -161,23 +137,23 @@ def tile_tsmixertimethenfeaturemixing_x2_kernel(
             h[u] = work.tile([P, 2, 4, P], F32, name="h", bufs=6)
             for k in (1, 0):
                 if on_s(u, k):
-                    i = 2 * half + k
-                    nc.scalar.activation(out=h[u][:, k], in_=perm(mt[u][k][:]), func=ACT.Relu, bias=bcol[:, i : i + 1], scale=1.0)
+                    j = 2 * half + k
+                    nc.scalar.activation(out=h[u][:, k], in_=perm(mt[u][k][:]), func=ACT.Relu, bias=bt[:, j : j + 1], scale=1.0)
 
         def res_g(u):
             b, half = divmod(u, 2)
             for k in (1, 0):
                 if on_s(u, k) and not on_p(u, k):
-                    i = 2 * half + k
-                    nc.gpsimd.tensor_tensor(out=h[u][:, k], in0=h[u][:, k], in1=perm(xr[b][:, i, :]), op=ALU.add)
+                    j = 2 * half + k
+                    nc.gpsimd.tensor_tensor(out=h[u][:, k], in0=h[u][:, k], in1=perm(xa[b][:, j, :]), op=ALU.add)
 
         def res_v(u):
             b, half = divmod(u, 2)
             for k in (0, 1):
                 if not on_s(u, k):
-                    i = 2 * half + k
+                    j = 2 * half + k
                     nc.vector.scalar_tensor_tensor(
-                        out=h[u][:, k], in0=perm(mt[u][k][:]), scalar=nbt[:, i : i + 1], in1=xb[u, k][:], op0=ALU.max, op1=ALU.add
+                        out=h[u][:, k], in0=perm(mt[u][k][:]), scalar=nbt[:, j : j + 1], in1=xb[u, k][:], op0=ALU.max, op1=ALU.add
                     )
 
         def trans_h(u, k):
@@ -185,7 +161,7 @@ def tile_tsmixertimethenfeaturemixing_x2_kernel(
             b, half = divmod(u, 2)
             if on_p(u, k):
                 for t in range(4):
-                    nc.tensor.matmul(th[u, k][:, t, :], lhsT=xr[b][:, 2 * half + k, t:C:4], rhs=identb[:], start=t == 0, stop=False)
+                    nc.tensor.matmul(th[u, k][:, t, :], lhsT=xa[b][:, 2 * half + k, t:C:4], rhs=identb[:], start=t == 0, stop=False)
             for t in range(4):
                 if on_p(u, k):
                     nc.tensor.matmul(th[u, k][:, t, :], lhsT=h[u][:, k, t, :], rhs=ident[:], start=False, stop=t == 3, is_transpose=True)
@@ -196,10 +172,7 @@ def tile_tsmixertimethenfeaturemixing_x2_kernel(
             if u not in hgi:
                 hgi[u] = work.tile([P, 2, P, 4], BF16, name="hgi", align_bytes=64)
             nc.vector.tensor_tensor(
-                out=hgi[u][:, k],
-                in0=th[u, k][:].rearrange("p t s -> p s t"),
-                in1=gc[:].unsqueeze(1).to_broadcast([P, P, 4]),
-                op=ALU.mult,
+                out=hgi[u][:, k], in0=th[u, k][:].rearrange("p t s -> p s t"), in1=gc[:].unsqueeze(1).to_broadcast([P, P, 4]), op=ALU.mult
             )
 
         def quant2(u):
@@ -224,20 +197,20 @@ def tile_tsmixertimethenfeaturemixing_x2_kernel(
                     )
                 qt[u].append(q)
 
-        def relu2(u, engs="SSSS"):
+        def relu2(u):
             r2[u] = work.tile([P, 4, 256], F32, name="r2", bufs=3)
             for i in range(4):
                 src = qt[u][i // 2][:, i % 2, :]
-                if engs[i] == "S":
-                    nc.scalar.activation(out=r2[u][:, i, :], in_=src, func=ACT.Relu, bias=bcol[:, 4 + i : 5 + i], scale=1.0)
+                if u == U - 1 and i >= 2:
+                    nc.vector.tensor_scalar(out=r2[u][:, i, :], in0=src, scalar1=bf[:, i : i + 1], scalar2=0.0, op0=ALU.add, op1=ALU.max)
                 else:
-                    nc.vector.tensor_scalar(out=r2[u][:, i, :], in0=src, scalar1=bcol[:, 4 + i : 5 + i], scalar2=0.0, op0=ALU.add, op1=ALU.max)
+                    nc.scalar.activation(out=r2[u][:, i, :], in_=src, func=ACT.Relu, bias=bf[:, i : i + 1], scale=1.0)
 
         def trans_r(u, k):
             tr[u, k] = psum.tile([P, 512], F32, name="tp")
             b, half = divmod(u, 2)
             if on_p(u, k):
-                nc.tensor.matmul(tr[u, k][:], lhsT=identb[:], rhs=xr[b][:, 2 * half + k, :], start=True, stop=False)
+                nc.tensor.matmul(tr[u, k][:], lhsT=identb[:], rhs=xa[b][:, 2 * half + k, :], start=True, stop=False)
             for i in range(4):
                 dst, src = tr[u, k][:, P * i : P * i + P], r2[u][:, i, P * k : P * k + P]
                 if on_p(u, k):
@@ -256,192 +229,189 @@ def tile_tsmixertimethenfeaturemixing_x2_kernel(
                 op=ALU.add,
             )
             if k == 1:
-                nc.sync.dma_start(out=out[b, 256 * half : 256 * half + 256, :].rearrange("(k p) c -> p k c", p=P), in_=ot[u][:])
+                nc.sync.dma_start(out=out[b].rearrange("(p j) c -> p j c", j=4)[:, 2 * half : 2 * half + 2, :], in_=ot[u][:])
 
-        def cast(u, k, on_vector=False):
+        def cast(u, k, eng):
             if u not in ob:
                 ob[u] = work.tile([P, 2, C], BF16, name="ob", bufs=3)
             dst = ob[u][:, k, :].rearrange("p (e c f) -> p e c f", e=2, f=2)
             src = ot[u][:, k, :].rearrange("p (c e f) -> p e c f", e=2, f=2)
-            if on_vector:
+            if eng == "V":
                 nc.vector.tensor_copy(out=dst, in_=src)
+            elif eng == "S":
+                nc.scalar.copy(out=dst, in_=src)
             else:
                 nc.gpsimd.tensor_scalar(out=dst, in0=src, scalar1=1.0, scalar2=0.0, op0=ALU.mult, op1=ALU.add)
 
         def trans_o(u, k):
-            if u == U - 1:
-                wtp[u, k] = psum.tile([P, 1, 2, P], F32, name="tp")
-            elif (u, 0) not in wtp:
-                wtp[u, 0] = psum.tile([P, 2, 2, P], F32, name="tp")
-            dst = wtp[u, k][:, 0] if u == U - 1 else wtp[u, 0][:, k]
+            if u not in wtp:
+                wtp[u] = psum.tile([P, 2, 2, P], F32, name="tp")
             words = ob[u][:, k, :].bitcast(F32)
             for e in range(2):
-                nc.tensor.transpose(dst[:, e, :], words[:, P * e : P * e + P], ident[:])
+                nc.tensor.transpose(wtp[u][:, k, e, :], words[:, P * e : P * e + P], ident[:])
 
         def pack_o(u):
             b, half = divmod(u, 2)
-            if half == 0:
+            if b not in oi:
                 oi[b] = work.tile([P, L, 2], F32, name="oi", align_bytes=64)
-            n = 1 if u == U - 1 else 2
-            for k in range(0, 2, n):
-                s0 = 256 * half + P * k
-                nc.scalar.copy(
-                    out=oi[b][:, s0 : s0 + P * n, :].rearrange("p (k s) e -> p k s e", k=n), in_=wtp[u, k][:].rearrange("p k e s -> p k s e")
-                )
+            nc.scalar.copy(
+                out=oi[b][:].rearrange("p (q j) e -> p q j e", j=4)[:, :, 2 * half : 2 * half + 2, :], in_=wtp[u][:].rearrange("p k e q -> p q k e")
+            )
 
-        def quant3(b, m0, m1):
-            if m0 == 0:
-                codes3[b] = work.tile([P, L], U32, name="codes3", bufs=3, align_bytes=64)
+        def quant3(b):
+            codes3[b] = work.tile([P, L], U32, name="codes3", bufs=3, align_bytes=64)
             nc.vector.quantize_mx(
-                out=codes3[b][:, m0:m1].bitcast(FP8X4),
-                scales=sc3[:, L * b + m0 : L * b + m1],
-                in_=oi[b][:, m0:m1, :].rearrange("p s e -> p (s e)").bitcast(BF16),
+                out=codes3[b][:].bitcast(FP8X4), scales=sc3[:, L * b : L * b + L], in_=oi[b][:].rearrange("p s e -> p (s e)").bitcast(BF16)
             )
-            w0 = 4 * L * b
             nc.sync.dma_start(
-                out=out_words[0].rearrange("p m t -> p (m t)")[:, w0 + 4 * m0 : w0 + 4 * m1].bitcast(I32), in_=codes3[b][:, m0:m1].bitcast(I32)
+                out=out_words[0].rearrange("p m t -> p (m t)")[:, 4 * L * b : 4 * L * b + 4 * L].bitcast(I32), in_=codes3[b][:].bitcast(I32)
             )
 
-        def store_scales(b0, b1):
-            for q in range(4):
-                nc.scalar.dma_start(
-                    out=out_scales[0, 4 * q : 4 * q + 4, L * b0 : L * b1].bitcast(I32), in_=sc3[32 * q : 32 * q + 4, L * b0 : L * b1].bitcast(I32)
-                )
-
-        def quantize_result(b, part):
-            if 0 <= b < B - 1 and part == 0:
-                quant3(b, 0, 512)
-            elif b == B - 1:
-                quant3(b, 256 * part, 256 * part + 256)
-
+        nc.gpsimd.memset(wts_raw[:].bitcast(I32), 0)
+        nc.vector.memset(rows[:], 0.0)
+        nc.vector.memset(wfs[:].bitcast(I32), 0)
+        make_identity(nc, identb[:])
+        make_identity(nc, ident[:])
+        nc.sync.dma_start(out=wt_raw[:].bitcast(I32), in_=w_t_words[0].bitcast(I32))
+        nc.scalar.dma_start(out=gt[:], in_=g_t.rearrange("(p j) -> p j", j=4))
+        for q in range(4):
+            nc.scalar.dma_start(out=wts_raw[32 * q : 32 * q + 4, :].bitcast(I32), in_=w_t_scales[0, 4 * q : 4 * q + 4, :].bitcast(I32))
+        nc.scalar.dma_start(out=bt16[:], in_=b_t.rearrange("(p j) -> p j", j=4))
+        nc.scalar.dma_start(out=rows[0:4, :], in_=b_f.rearrange("(i p) -> i p", p=P))
+        load_half(0)
+        load_half(1)
+        load_x(0)
+        nc.scalar.dma_start(out=gc[:], in_=g_c.rearrange("(p j) -> p j", j=4))
+        load_x(1)
+        nc.sync.dma_start(out=wf[:].bitcast(I32), in_=w_f_words[0].bitcast(I32))
+        for q in range(4):
+            nc.scalar.dma_start(out=wfs[32 * q : 32 * q + 4, :].bitcast(I32), in_=w_f_scales[0, 4 * q : 4 * q + 4, :].bitcast(I32))
+        load_x(2)
         vt = psum.tile([P, P], BF16, name="tp")
 
         with tc.manual_schedule():
+            nc.vector.tensor_copy(out=wt[:].rearrange("p (j q e) -> p q j e", j=4, e=2), in_=wt_raw[:].rearrange("p (q j e) -> p q j e", j=4, e=2))
             mult(0, 0)
-            interleave(0, 0, 96, True)
-            interleave(0, 96, 256, False)
-            nc.tensor.transpose(vt[:], rows[:], identb[:])
-            nc.vector.tensor_copy(out=bcol[:], in_=vt[:, 0:8])
+            interleave(0, 0, 96, "S")
+            interleave(0, 96, 256, "V")
+            nc.vector.tensor_copy(out=wts[:].rearrange("p (j q) -> p q j", j=4), in_=wts_raw[:].rearrange("p (q j) -> p q j", j=4))
             mult(0, 1)
-            interleave(0, 256, 352, True)
-            nc.vector.tensor_scalar_mul(out=nbt[:], in0=bcol[:, 0:4], scalar1=-1.0)
-            interleave(0, 352, 512, False)
+            interleave(0, 256, 352, "S")
+            nc.vector.tensor_copy(out=bt[:], in_=bt16[:])
+            nc.vector.tensor_scalar_mul(out=nbt[:], in0=bt[:], scalar1=-1.0)
+            interleave(0, 352, 512, "V")
             quant1(0, 0, 256)
             quant1(0, 256, 512)
+            nc.tensor.transpose(vt[:], rows[:], identb[:])
             bias_res(0)
+            bias_res(1)
             mx1(0)
             relu_s(0)
             res_v(0)
-            bias_res(1)
             res_g(0)
             mx1(1)
             relu_s(1)
-            res_v(1)
-            res_g(1)
-            mult(1, 0)
-            mult(1, 1)
-            load_x(2)
+            nc.vector.tensor_copy(out=bf[:], in_=vt[:, 0:4])
             trans_h(0, 0)
             trans_h(0, 1)
-            for r in range(-1, B + 4):
-                if 1 <= r < B:
-                    interleave(r, 256, 512, True)
-                if 0 <= 2 * r - 3 < U:
-                    relu2(2 * r - 3)
-                if 1 <= 2 * r - 2 < U:
-                    trans_h(2 * r - 2, 1)
+            for r in range(-3, B + 4):
+                if 1 <= 2 * r < U:
+                    trans_h(2 * r, 0)
                 if 0 <= 2 * r - 4 < U:
-                    outs(2 * r - 4, 0)
-                if 0 <= 2 * r - 5 < U:
-                    trans_o(2 * r - 5, 0)
-                if 2 <= r + 1 < B:
-                    load_res(r + 1)
-                if 2 <= r + 1 < B:
-                    mult(r + 1, 0)
-                if 0 <= 2 * r - 4 < U:
-                    outs(2 * r - 4, 1)
-                quantize_result(r - 4, 1)
-                if 0 <= 2 * r - 4 < U:
-                    cast(2 * r - 4, 1, 2 * r - 4 >= U - 2)
-                if 1 <= 2 * r - 2 < U:
-                    trans_h(2 * r - 2, 0)
-                if 3 <= r + 4 < B:
-                    load_x(r + 4)
-                if 0 <= 2 * r - 5 < U:
-                    pack_o(2 * r - 5)
-                if 0 <= 2 * r - 2 < U:
-                    hg(2 * r - 2, 1)
-                if 0 <= 2 * r - 2 < U:
-                    hg(2 * r - 2, 0)
-                quantize_result(r - 3, 0)
-                if 0 <= 2 * r - 3 < U:
-                    trans_r(2 * r - 3, 0)
-                if 2 <= 2 * r - 1 < U:
-                    mx1(2 * r - 1)
-                if 0 <= 2 * r - 2 < U:
-                    quant2(2 * r - 2)
-                if 0 <= 2 * r - 4 < U:
-                    trans_o(2 * r - 4, 1)
-                if 1 <= r < B:
-                    quant1(r)
-                if 1 <= r + 1 < B:
-                    interleave(r + 1, 0, 256, True)
-                if 0 <= 2 * r - 4 < U:
-                    cast(2 * r - 4, 0, 2 * r - 4 >= U - 2)
-                if 2 <= 2 * r - 1 < U:
-                    relu_s(2 * r - 1)
-                if 0 <= 2 * r - 2 < U:
-                    mx2(2 * r - 2)
-                if 2 <= 2 * r - 1 < U:
-                    res_v(2 * r - 1)
-                if 0 <= 2 * r - 3 < U:
-                    trans_r(2 * r - 3, 1)
-                if 1 <= 2 * r - 1 < U:
-                    trans_h(2 * r - 1, 0)
-                if 2 <= 2 * r - 1 < U:
-                    res_g(2 * r - 1)
-                if 2 <= 2 * r + 1 < U:
-                    bias_res(2 * r + 1)
-                if 0 <= 2 * r - 3 < U:
-                    outs(2 * r - 3, 0)
-                if 0 <= 2 * r - 4 < U:
-                    trans_o(2 * r - 4, 0)
-                if 0 <= 2 * r - 3 < U:
-                    outs(2 * r - 3, 1)
-                if 1 <= 2 * r - 1 < U:
-                    trans_h(2 * r - 1, 1)
-                if 0 <= 2 * r - 3 < U:
-                    cast(2 * r - 3, 0, 2 * r - 3 >= U - 2)
-                if 0 <= 2 * r - 2 < U:
-                    relu2(2 * r - 2)
-                if 0 <= 2 * r - 1 < U:
-                    hg(2 * r - 1, 0)
-                if 0 <= 2 * r - 1 < U:
-                    hg(2 * r - 1, 1)
-                if 2 <= r + 2 < B:
-                    mult(r + 2, 1)
-                if 0 <= 2 * r - 3 < U:
-                    cast(2 * r - 3, 1, 2 * r - 3 >= U - 2)
-                if 2 <= 2 * r < U:
-                    mx1(2 * r)
-                if 0 <= 2 * r - 4 < U:
-                    pack_o(2 * r - 4)
-                if 0 <= 2 * r - 1 < U:
-                    quant2(2 * r - 1)
-                if 2 <= 2 * r < U:
-                    bias_res(2 * r)
-                if 2 <= 2 * r < U:
-                    relu_s(2 * r)
+                    cast(2 * r - 4, 0, "V" if 2 * r - 4 >= U - 2 else "G")
                 if 0 <= 2 * r - 2 < U:
                     trans_r(2 * r - 2, 0)
-                if 2 <= 2 * r < U:
-                    res_v(2 * r)
-                if 0 <= 2 * r - 2 < U:
-                    trans_r(2 * r - 2, 1)
-                if 2 <= 2 * r < U:
-                    res_g(2 * r)
+                if 0 <= 2 * r - 4 < U:
+                    trans_o(2 * r - 4, 0)
+                if 0 <= 2 * r - 5 < U:
+                    pack_o(2 * r - 5)
                 if 0 <= 2 * r - 3 < U:
-                    trans_o(2 * r - 3, 1)
+                    outs(2 * r - 3, 0)
+                if 2 <= 2 * r + 1 < U:
+                    relu_s(2 * r + 1)
+                if 1 <= r + 1 < B:
+                    interleave(r + 1, 256, 512, "S")
+                if 0 <= 2 * r - 1 < U:
+                    quant2(2 * r - 1)
+                if 0 <= 2 * r - 4 < U:
+                    trans_o(2 * r - 4, 1)
+                if 0 <= 2 * r - 3 < U:
+                    trans_r(2 * r - 3, 1)
+                if 1 <= 2 * r + 1 < U:
+                    res_v(2 * r + 1)
                 if 0 <= 2 * r - 1 < U:
                     mx2(2 * r - 1)
-            store_scales(0, B)
+                if 1 <= 2 * r + 1 < U:
+                    res_g(2 * r + 1)
+                if 0 <= 2 * r < U:
+                    hg(2 * r, 1)
+                if 0 <= 2 * r < U:
+                    hg(2 * r, 0)
+                if 0 <= 2 * r - 2 < U:
+                    trans_r(2 * r - 2, 1)
+                if 0 <= 2 * r - 2 < U:
+                    outs(2 * r - 2, 0)
+                if 0 <= r - 3 < B:
+                    quant3(r - 3)
+                if 1 <= 2 * r + 1 < U:
+                    trans_h(2 * r + 1, 1)
+                if 1 <= r + 1 < B:
+                    interleave(r + 1, 0, 256, "S")
+                if 1 <= 2 * r + 1 < U:
+                    trans_h(2 * r + 1, 0)
+                if 0 <= 2 * r - 4 < U:
+                    pack_o(2 * r - 4)
+                if 0 <= 2 * r < U:
+                    quant2(2 * r)
+                if 0 <= 2 * r < U:
+                    mx2(2 * r)
+                if 2 <= 2 * r + 3 < U:
+                    bias_res(2 * r + 3)
+                if 1 <= r + 3 < B:
+                    mult(r + 3, 1)
+                if 3 <= r + 6 < B:
+                    load_x(r + 6)
+                if 1 <= r + 1 < B:
+                    quant1(r + 1)
+                if 1 <= r + 3 < B:
+                    mult(r + 3, 0)
+                if 2 <= 2 * r + 2 < U:
+                    mx1(2 * r + 2)
+                if 0 <= 2 * r - 3 < U:
+                    cast(2 * r - 3, 0, "V" if 2 * r - 3 >= U - 2 else "G")
+                if 0 <= 2 * r - 3 < U:
+                    outs(2 * r - 3, 1)
+                if 0 <= 2 * r - 3 < U:
+                    trans_o(2 * r - 3, 0)
+                if 0 <= 2 * r - 1 < U:
+                    relu2(2 * r - 1)
+                if 0 <= 2 * r < U:
+                    relu2(2 * r)
+                if 0 <= 2 * r - 1 < U:
+                    trans_r(2 * r - 1, 0)
+                if 0 <= 2 * r - 3 < U:
+                    cast(2 * r - 3, 1, "V" if 2 * r - 3 >= U - 2 else "G")
+                if 0 <= 2 * r - 2 < U:
+                    outs(2 * r - 2, 1)
+                if 0 <= 2 * r - 3 < U:
+                    trans_o(2 * r - 3, 1)
+                if 2 <= 2 * r + 2 < U:
+                    bias_res(2 * r + 2)
+                if 0 <= 2 * r - 2 < U:
+                    cast(2 * r - 2, 1, "V" if 2 * r - 2 >= U - 2 else "G")
+                if 2 <= 2 * r + 3 < U:
+                    mx1(2 * r + 3)
+                if 1 <= 2 * r + 26 < U:
+                    res_g(2 * r + 26)
+                if 2 <= 2 * r + 2 < U:
+                    relu_s(2 * r + 2)
+                if 0 <= 2 * r + 1 < U:
+                    hg(2 * r + 1, 1)
+                if 0 <= 2 * r + 1 < U:
+                    hg(2 * r + 1, 0)
+                if 1 <= 2 * r + 2 < U:
+                    res_v(2 * r + 2)
+                if 1 <= 2 * r + 2 < U:
+                    trans_h(2 * r + 2, 1)
+            for q in range(4):
+                nc.scalar.dma_start(out=out_scales[0, 4 * q : 4 * q + 4, :].bitcast(I32), in_=sc3[32 * q : 32 * q + 4, :].bitcast(I32))

@@ -50,10 +50,10 @@ def tile_tsmixertimethenfeaturemixing_x2_kernel(
         qt, r2, tr, ot, ob, wtp, oi, codes3 = {}, {}, {}, {}, {}, {}, {}, {}
 
         def on_p(u, k):
-            return k == 1 and u % 4 != 3
+            return k == 1 and u % 2 == 0
 
         def on_s(u, k):
-            return on_p(u, k) or k == 1 or u % 4 == 1
+            return on_p(u, k) or k == 1
 
         def perm(ap):
             return ap.rearrange("p (c t) -> p t c", t=4)
@@ -125,7 +125,7 @@ def tile_tsmixertimethenfeaturemixing_x2_kernel(
                 if not on_s(u, k):
                     j = 2 * half + k
                     xb[u, k] = work.tile([P, 4, P], F32, name="xb", bufs=3)
-                    if False:
+                    if True:
                         nc.scalar.activation(out=xb[u, k][:], in_=perm(xa[b][:, j, :]), func=ACT.Identity, bias=bt[:, j : j + 1], scale=1.0)
                     else:
                         nc.gpsimd.tensor_scalar(
@@ -134,7 +134,8 @@ def tile_tsmixertimethenfeaturemixing_x2_kernel(
 
         def relu_s(u):
             b, half = divmod(u, 2)
-            h[u] = work.tile([P, 2, 4, P], F32, name="h", bufs=6)
+            if u not in h:
+                h[u] = work.tile([P, 2, 4, P], F32, name="h", bufs=6)
             for k in (1, 0):
                 if on_s(u, k):
                     j = 2 * half + k
@@ -149,6 +150,8 @@ def tile_tsmixertimethenfeaturemixing_x2_kernel(
 
         def res_v(u):
             b, half = divmod(u, 2)
+            if u not in h:
+                h[u] = work.tile([P, 2, 4, P], F32, name="h", bufs=6)
             for k in (0, 1):
                 if not on_s(u, k):
                     j = 2 * half + k
@@ -231,7 +234,8 @@ def tile_tsmixertimethenfeaturemixing_x2_kernel(
             if k == 1:
                 nc.sync.dma_start(out=out[b].rearrange("(p j) c -> p j c", j=4)[:, 2 * half : 2 * half + 2, :], in_=ot[u][:])
 
-        def cast(u, k, eng):
+        def cast(u, k):
+            eng = "V" if u >= U - 2 else "G"
             if u not in ob:
                 ob[u] = work.tile([P, 2, C], BF16, name="ob", bufs=3)
             dst = ob[u][:, k, :].rearrange("p (e c f) -> p e c f", e=2, f=2)
@@ -315,103 +319,101 @@ def tile_tsmixertimethenfeaturemixing_x2_kernel(
             trans_h(0, 0)
             trans_h(0, 1)
             for r in range(-3, B + 4):
-                if 1 <= 2 * r < U:
-                    trans_h(2 * r, 0)
-                if 0 <= 2 * r - 4 < U:
-                    cast(2 * r - 4, 0, "V" if 2 * r - 4 >= U - 2 else "G")
-                if 0 <= 2 * r - 2 < U:
-                    trans_r(2 * r - 2, 0)
-                if 0 <= 2 * r - 4 < U:
-                    trans_o(2 * r - 4, 0)
-                if 0 <= 2 * r - 5 < U:
-                    pack_o(2 * r - 5)
-                if 0 <= 2 * r - 3 < U:
-                    outs(2 * r - 3, 0)
-                if 2 <= 2 * r + 1 < U:
-                    relu_s(2 * r + 1)
-                if 1 <= r + 1 < B:
-                    interleave(r + 1, 256, 512, "S")
-                if 0 <= 2 * r - 1 < U:
-                    quant2(2 * r - 1)
-                if 0 <= 2 * r - 4 < U:
-                    trans_o(2 * r - 4, 1)
-                if 0 <= 2 * r - 3 < U:
-                    trans_r(2 * r - 3, 1)
-                if 1 <= 2 * r + 1 < U:
-                    res_v(2 * r + 1)
-                if 0 <= 2 * r - 1 < U:
-                    mx2(2 * r - 1)
-                if 1 <= 2 * r + 1 < U:
-                    res_g(2 * r + 1)
-                if 0 <= 2 * r < U:
-                    hg(2 * r, 1)
-                if 0 <= 2 * r < U:
-                    hg(2 * r, 0)
-                if 0 <= 2 * r - 2 < U:
-                    trans_r(2 * r - 2, 1)
-                if 0 <= 2 * r - 2 < U:
-                    outs(2 * r - 2, 0)
-                if 0 <= r - 3 < B:
-                    quant3(r - 3)
-                if 1 <= 2 * r + 1 < U:
-                    trans_h(2 * r + 1, 1)
                 if 1 <= r + 1 < B:
                     interleave(r + 1, 0, 256, "S")
-                if 1 <= 2 * r + 1 < U:
-                    trans_h(2 * r + 1, 0)
-                if 0 <= 2 * r - 4 < U:
-                    pack_o(2 * r - 4)
-                if 0 <= 2 * r < U:
-                    quant2(2 * r)
-                if 0 <= 2 * r < U:
-                    mx2(2 * r)
-                if 2 <= 2 * r + 3 < U:
-                    bias_res(2 * r + 3)
-                if 1 <= r + 3 < B:
-                    mult(r + 3, 1)
-                if 3 <= r + 6 < B:
-                    load_x(r + 6)
-                if 1 <= r + 1 < B:
-                    quant1(r + 1)
-                if 1 <= r + 3 < B:
-                    mult(r + 3, 0)
-                if 2 <= 2 * r + 2 < U:
-                    mx1(2 * r + 2)
-                if 0 <= 2 * r - 3 < U:
-                    cast(2 * r - 3, 0, "V" if 2 * r - 3 >= U - 2 else "G")
-                if 0 <= 2 * r - 3 < U:
-                    outs(2 * r - 3, 1)
-                if 0 <= 2 * r - 3 < U:
-                    trans_o(2 * r - 3, 0)
-                if 0 <= 2 * r - 1 < U:
-                    relu2(2 * r - 1)
-                if 0 <= 2 * r < U:
-                    relu2(2 * r)
-                if 0 <= 2 * r - 1 < U:
-                    trans_r(2 * r - 1, 0)
-                if 0 <= 2 * r - 3 < U:
-                    cast(2 * r - 3, 1, "V" if 2 * r - 3 >= U - 2 else "G")
                 if 0 <= 2 * r - 2 < U:
-                    outs(2 * r - 2, 1)
-                if 0 <= 2 * r - 3 < U:
-                    trans_o(2 * r - 3, 1)
+                    outs(2 * r - 2, 0)
+                if 0 <= 2 * r - 1 < U:
+                    mx2(2 * r - 1)
                 if 2 <= 2 * r + 2 < U:
                     bias_res(2 * r + 2)
                 if 0 <= 2 * r - 2 < U:
-                    cast(2 * r - 2, 1, "V" if 2 * r - 2 >= U - 2 else "G")
-                if 2 <= 2 * r + 3 < U:
-                    mx1(2 * r + 3)
-                if 1 <= 2 * r + 26 < U:
-                    res_g(2 * r + 26)
-                if 2 <= 2 * r + 2 < U:
-                    relu_s(2 * r + 2)
+                    trans_r(2 * r - 2, 1)
+                if 0 <= 2 * r < U:
+                    quant2(2 * r)
+                if 0 <= 2 * r - 4 < U:
+                    trans_o(2 * r - 4, 0)
+                if 1 <= r + 2 < B:
+                    mult(r + 2, 1)
+                if 0 <= 2 * r - 3 < U:
+                    cast(2 * r - 3, 1)
+                if 0 <= 2 * r - 2 < U:
+                    outs(2 * r - 2, 1)
+                if 1 <= 2 * r + 1 < U:
+                    trans_h(2 * r + 1, 0)
+                if 0 <= 2 * r - 1 < U:
+                    relu2(2 * r - 1)
+                if 1 <= 2 * r + 1 < U:
+                    trans_h(2 * r + 1, 1)
+                if 1 <= r + 1 < B:
+                    quant1(r + 1)
+                if 0 <= 2 * r < U:
+                    mx2(2 * r)
                 if 0 <= 2 * r + 1 < U:
                     hg(2 * r + 1, 1)
+                if 2 <= 2 * r + 2 < U:
+                    mx1(2 * r + 2)
+                if 0 <= 2 * r - 4 < U:
+                    pack_o(2 * r - 4)
+                if 0 <= 2 * r - 3 < U:
+                    trans_o(2 * r - 3, 0)
                 if 0 <= 2 * r + 1 < U:
                     hg(2 * r + 1, 0)
+                if 0 <= 2 * r - 3 < U:
+                    trans_o(2 * r - 3, 1)
+                if 0 <= 2 * r - 1 < U:
+                    trans_r(2 * r - 1, 0)
+                if 0 <= 2 * r < U:
+                    relu2(2 * r)
+                if 0 <= 2 * r - 1 < U:
+                    trans_r(2 * r - 1, 1)
                 if 1 <= 2 * r + 2 < U:
                     res_v(2 * r + 2)
+                if 1 <= r + 2 < B:
+                    mult(r + 2, 0)
+                if 0 <= 2 * r - 3 < U:
+                    pack_o(2 * r - 3)
+                if 2 <= 2 * r + 2 < U:
+                    relu_s(2 * r + 2)
+                if 0 <= 2 * r - 2 < U:
+                    cast(2 * r - 2, 1)
+                if 0 <= 2 * r + 1 < U:
+                    quant2(2 * r + 1)
+                if 0 <= 2 * r - 1 < U:
+                    outs(2 * r - 1, 0)
+                if 2 <= 2 * r + 3 < U:
+                    bias_res(2 * r + 3)
+                if 2 <= 2 * r + 3 < U:
+                    mx1(2 * r + 3)
+                if 0 <= r - 2 < B:
+                    quant3(r - 2)
+                if 0 <= 2 * r - 2 < U:
+                    cast(2 * r - 2, 0)
+                if 2 <= 2 * r + 3 < U:
+                    relu_s(2 * r + 3)
+                if 0 <= 2 * r - 1 < U:
+                    outs(2 * r - 1, 1)
                 if 1 <= 2 * r + 2 < U:
                     trans_h(2 * r + 2, 1)
+                if 1 <= r + 2 < B:
+                    interleave(r + 2, 256, 512, "S")
+                if 1 <= 2 * r + 3 < U:
+                    res_v(2 * r + 3)
+                if 1 <= 2 * r + 2 < U:
+                    trans_h(2 * r + 2, 0)
+                if 0 <= 2 * r - 2 < U:
+                    trans_o(2 * r - 2, 1)
+                if 0 <= 2 * r < U:
+                    trans_r(2 * r, 0)
+                if 0 <= 2 * r + 2 < U:
+                    hg(2 * r + 2, 0)
+                if 0 <= 2 * r - 1 < U:
+                    cast(2 * r - 1, 0)
+                if 0 <= 2 * r + 2 < U:
+                    hg(2 * r + 2, 1)
+                if 3 <= r + 5 < B:
+                    load_x(r + 5)
+                if 1 <= 2 * r + 3 < U:
+                    res_g(2 * r + 3)
             for q in range(4):
                 nc.scalar.dma_start(out=out_scales[0, 4 * q : 4 * q + 4, :].bitcast(I32), in_=sc3[32 * q : 32 * q + 4, :].bitcast(I32))

from contextlib import ExitStack

import concourse.mybir as mybir
from concourse.masks import make_identity

F32 = mybir.dt.float32
BF16 = mybir.dt.bfloat16
I32 = mybir.dt.int32
U32 = mybir.dt.uint32
U8 = mybir.dt.uint8
FP8X4 = mybir.dt.float8_e4m3fn_x4
FP4X4 = mybir.dt.float4_e2m1fn_x4
ALU = mybir.AluOpType
ACT = mybir.ActivationFunctionType

B, L, C = 8, 512, 512
P = 128
U = 2 * B
FLOPS = 2 * 2 * B * L * C * C


def tile_tsmixertimethenfeaturemixing_x2_kernel(
    tc, x, g_t, w_t_words, w_t_scales, b_t, g_c, w_f_words, w_f_scales, b_f, out, out_words, out_scales
):
    nc = tc.nc
    with ExitStack() as ctx:
        keep = ctx.enter_context(tc.tile_pool(name="keep", bufs=1))
        work = ctx.enter_context(tc.tile_pool(name="work", bufs=2))
        psum = ctx.enter_context(tc.psum_pool(name="psum", bufs=4))

        gt = keep.tile([P, 4], BF16, name="gt")
        gc = keep.tile([P, 4], BF16, name="gc")
        bt16 = keep.tile([P, 4], BF16, name="bt16")
        rows = keep.tile([P, P], BF16, name="rows")
        wt_raw = keep.tile([P, 2 * L], U8, name="wt_raw", align_bytes=64)
        wts_raw = keep.tile([P, L], U8, name="wts_raw", align_bytes=64)
        wt = keep.tile([P, 2 * L], U8, name="wt", align_bytes=64)
        wts = keep.tile([P, L], U8, name="wts", align_bytes=64)
        wf = keep.tile([P, 2 * C], U8, name="wf", align_bytes=64)
        wfs = keep.tile([P, C], U8, name="wfs", align_bytes=64)
        ident = keep.tile([P, P], F32, name="ident")
        identb = keep.tile([P, P], BF16, name="identb")
        bt = keep.tile([P, 4], F32, name="bt")
        nbt = keep.tile([P, 4], F32, name="nbt")
        bf = keep.tile([P, 4], F32, name="bf")
        sc3 = keep.tile([P, B * L], U8, name="sc3", align_bytes=64)

        xa, xg, grouped, codes1, scale1 = {}, {}, {}, {}, {}
        mt, h, xb, th, hgi, codes2, scale2 = {}, {}, {}, {}, {}, {}, {}
        qt, r2, tr, ot, ob, wtp, oi, codes3 = {}, {}, {}, {}, {}, {}, {}, {}

        def on_p(u, k):
            return k == 1 and u % 2 == 0

        def on_s(u, k):
            return on_p(u, k) or k == 1

        def perm(ap):
            return ap.rearrange("p (c t) -> p t c", t=4)

        def load_half(part):
            xa[0, part] = work.tile([P, 4, C // 2], BF16, name="xa0", bufs=2)
            c = slice(part * C // 2, (part + 1) * C // 2)
            nc.sync.dma_start(out=xa[0, part][:], in_=x[0, :, c].rearrange("(p j) c -> p j c", j=4))

        def load_x(b):
            xa[b] = work.tile([P, 4, C], BF16, name="xa", bufs=7)
            nc.sync.dma_start(out=xa[b][:], in_=x[b].rearrange("(p j) c -> p j c", j=4))

        def mult(b, part):
            if b == 0:
                xg[0, part] = work.tile([P, 4, C // 2], BF16, name="xg0", bufs=2, align_bytes=64)
                src, dst, js = xa[0, part], xg[0, part], (0, 1, 2, 3)
            else:
                if b not in xg:
                    xg[b] = work.tile([P, 4, C], BF16, name="xg", bufs=4, align_bytes=64)
                src, dst, js = xa[b], xg[b], (2 * part, 2 * part + 1)
            for j in js:
                nc.vector.tensor_scalar_mul(out=dst[:, j, :], in0=src[:, j, :], scalar1=gt[:, j : j + 1])

        def interleave(b, c0, c1, eng):
            if b not in grouped:
                grouped[b] = work.tile([P, C, 4], BF16, name="grouped", bufs=4, align_bytes=64)
            if b == 0:
                part, off = divmod(c0, C // 2)
                src = xg[0, part][:, :, off : off + c1 - c0].rearrange("p j c -> p c j")
            else:
                src = xg[b][:, :, c0:c1].rearrange("p j c -> p c j")
            dst = grouped[b][:, c0:c1, :]
            if eng == "S":
                nc.scalar.copy(out=dst, in_=src)
            elif eng == "G":
                nc.gpsimd.tensor_scalar(out=dst, in0=src, scalar1=1.0, scalar2=0.0, op0=ALU.mult, op1=ALU.add)
            else:
                nc.vector.tensor_copy(out=dst, in_=src)

        def quant1(b, c0=0, c1=C):
            if b not in codes1:
                codes1[b] = work.tile([P, C], U32, name="codes1", bufs=4, align_bytes=64)
                scale1[b] = work.tile([P, C], U8, name="scale1", bufs=4, align_bytes=64)
            nc.vector.quantize_mx(
                out=codes1[b][:, c0:c1].bitcast(FP8X4), scales=scale1[b][:, c0:c1], in_=grouped[b][:, c0:c1, :].rearrange("p c j -> p (c j)")
            )

        def mx1(u):
            b, half = divmod(u, 2)
            mt[u] = {k: psum.tile([P, 512], F32, name="mx") for k in (1, 0)}
            step = 256 if u == 0 else C
            for c0 in range(0, C, step):
                for k in (1, 0):
                    j = 2 * half + k
                    nc.tensor.matmul_mx(
                        out=mt[u][k][:, c0 : c0 + step],
                        lhsT=wt[:, 256 * j : 256 * j + 256].bitcast(FP4X4),
                        lhsT_scale=wts[:, P * j : P * j + P],
                        rhs=codes1[b][:, c0 : c0 + step].bitcast(FP8X4),
                        rhs_scale=scale1[b][:, c0 : c0 + step],
                        start=True,
                        stop=True,
                    )

        def bias_res(u):
            b, half = divmod(u, 2)
            for k in (0, 1):
                if not on_s(u, k):
                    j = 2 * half + k
                    xb[u, k] = work.tile([P, 4, P], F32, name="xb", bufs=3)
                    if True:
                        nc.scalar.activation(out=xb[u, k][:], in_=perm(xa[b][:, j, :]), func=ACT.Identity, bias=bt[:, j : j + 1], scale=1.0)
                    else:
                        nc.gpsimd.tensor_scalar(
                            out=xb[u, k][:], in0=perm(xa[b][:, j, :]), scalar1=1.0, scalar2=bt[:, j : j + 1], op0=ALU.mult, op1=ALU.add
                        )

        def relu_s(u):
            b, half = divmod(u, 2)
            if u not in h:
                h[u] = work.tile([P, 2, 4, P], F32, name="h", bufs=6)
            for k in (1, 0):
                if on_s(u, k):
                    j = 2 * half + k
                    nc.scalar.activation(out=h[u][:, k], in_=perm(mt[u][k][:]), func=ACT.Relu, bias=bt[:, j : j + 1], scale=1.0)

        def res_g(u):
            b, half = divmod(u, 2)
            for k in (1, 0):
                if on_s(u, k) and not on_p(u, k):
                    j = 2 * half + k
                    nc.gpsimd.tensor_tensor(out=h[u][:, k], in0=h[u][:, k], in1=perm(xa[b][:, j, :]), op=ALU.add)

        def res_v(u):
            b, half = divmod(u, 2)
            if u not in h:
                h[u] = work.tile([P, 2, 4, P], F32, name="h", bufs=6)
            for k in (0, 1):
                if not on_s(u, k):
                    j = 2 * half + k
                    nc.vector.scalar_tensor_tensor(
                        out=h[u][:, k], in0=perm(mt[u][k][:]), scalar=nbt[:, j : j + 1], in1=xb[u, k][:], op0=ALU.max, op1=ALU.add
                    )

        def trans_h(u, k):
            th[u, k] = psum.tile([P, 4, P], F32, name="tp")
            b, half = divmod(u, 2)
            if on_p(u, k):
                for t in range(4):
                    nc.tensor.matmul(th[u, k][:, t, :], lhsT=xa[b][:, 2 * half + k, t:C:4], rhs=identb[:], start=t == 0, stop=False)
            for t in range(4):
                if on_p(u, k):
                    nc.tensor.matmul(th[u, k][:, t, :], lhsT=h[u][:, k, t, :], rhs=ident[:], start=False, stop=t == 3, is_transpose=True)
                else:
                    nc.tensor.transpose(th[u, k][:, t, :], h[u][:, k, t, :], ident[:])

        def hg(u, k):
            if u not in hgi:
                hgi[u] = work.tile([P, 2, P, 4], BF16, name="hgi", align_bytes=64)
            nc.vector.tensor_tensor(
                out=hgi[u][:, k], in0=th[u, k][:].rearrange("p t s -> p s t"), in1=gc[:].unsqueeze(1).to_broadcast([P, P, 4]), op=ALU.mult
            )

        def quant2(u):
            codes2[u] = work.tile([P, 256], U32, name="codes2", align_bytes=64)
            scale2[u] = work.tile([P, 256], U8, name="scale2", align_bytes=64)
            nc.vector.quantize_mx(out=codes2[u][:].bitcast(FP8X4), scales=scale2[u][:], in_=hgi[u][:].rearrange("p k s t -> p (k s t)"))

        def mx2(u):
            qt[u] = []
            for d in range(2):
                q = psum.tile([P, 2, 256], F32, name="mx")
                for e in range(2):
                    i = 2 * d + e
                    nc.tensor.matmul_mx(
                        out=q[:, e, :],
                        lhsT=wf[:, 256 * i : 256 * i + 256].bitcast(FP4X4),
                        lhsT_scale=wfs[:, P * i : P * i + P],
                        rhs=codes2[u][:].bitcast(FP8X4),
                        rhs_scale=scale2[u][:],
                        start=True,
                        stop=True,
                    )
                qt[u].append(q)

        def relu2(u):
            r2[u] = work.tile([P, 4, 256], F32, name="r2", bufs=3)
            for i in range(4):
                src = qt[u][i // 2][:, i % 2, :]
                if u == U - 1 and i >= 2:
                    nc.vector.tensor_scalar(out=r2[u][:, i, :], in0=src, scalar1=bf[:, i : i + 1], scalar2=0.0, op0=ALU.add, op1=ALU.max)
                else:
                    nc.scalar.activation(out=r2[u][:, i, :], in_=src, func=ACT.Relu, bias=bf[:, i : i + 1], scale=1.0)

        def trans_r(u, k):
            tr[u, k] = psum.tile([P, 512], F32, name="tp")
            b, half = divmod(u, 2)
            if on_p(u, k):
                nc.tensor.matmul(tr[u, k][:], lhsT=identb[:], rhs=xa[b][:, 2 * half + k, :], start=True, stop=False)
            for i in range(4):
                dst, src = tr[u, k][:, P * i : P * i + P], r2[u][:, i, P * k : P * k + P]
                if on_p(u, k):
                    nc.tensor.matmul(dst, lhsT=src, rhs=ident[:], start=False, stop=i == 3, is_transpose=True)
                else:
                    nc.tensor.transpose(dst, src, ident[:])

        def outs(u, k):
            b, half = divmod(u, 2)
            if u not in ot:
                ot[u] = work.tile([P, 2, C], F32, name="ot", bufs=4)
            nc.vector.tensor_tensor(
                out=ot[u][:, k, :].rearrange("p (c t) -> p c t", t=4),
                in0=tr[u, k][:].rearrange("p (c t) -> p c t", t=4),
                in1=h[u][:, k].rearrange("p t c -> p c t"),
                op=ALU.add,
            )
            if k == 1:
                nc.sync.dma_start(out=out[b].rearrange("(p j) c -> p j c", j=4)[:, 2 * half : 2 * half + 2, :], in_=ot[u][:])

        def cast(u, k):
            eng = "V" if u >= U - 2 else "G"
            if u not in ob:
                ob[u] = work.tile([P, 2, C], BF16, name="ob", bufs=3)
            dst = ob[u][:, k, :].rearrange("p (e c f) -> p e c f", e=2, f=2)
            src = ot[u][:, k, :].rearrange("p (c e f) -> p e c f", e=2, f=2)
            if eng == "V":
                nc.vector.tensor_copy(out=dst, in_=src)
            elif eng == "S":
                nc.scalar.copy(out=dst, in_=src)
            else:
                nc.gpsimd.tensor_scalar(out=dst, in0=src, scalar1=1.0, scalar2=0.0, op0=ALU.mult, op1=ALU.add)

        def trans_o(u, k):
            if u not in wtp:
                wtp[u] = psum.tile([P, 2, 2, P], F32, name="tp")
            words = ob[u][:, k, :].bitcast(F32)
            for e in range(2):
                nc.tensor.transpose(wtp[u][:, k, e, :], words[:, P * e : P * e + P], ident[:])

        def pack_o(u):
            b, half = divmod(u, 2)
            if b not in oi:
                oi[b] = work.tile([P, L, 2], F32, name="oi", align_bytes=64)
            nc.scalar.copy(
                out=oi[b][:].rearrange("p (q j) e -> p q j e", j=4)[:, :, 2 * half : 2 * half + 2, :], in_=wtp[u][:].rearrange("p k e q -> p q k e")
            )

        def quant3(b):
            codes3[b] = work.tile([P, L], U32, name="codes3", bufs=3, align_bytes=64)
            nc.vector.quantize_mx(
                out=codes3[b][:].bitcast(FP8X4), scales=sc3[:, L * b : L * b + L], in_=oi[b][:].rearrange("p s e -> p (s e)").bitcast(BF16)
            )
            nc.sync.dma_start(
                out=out_words[0].rearrange("p m t -> p (m t)")[:, 4 * L * b : 4 * L * b + 4 * L].bitcast(I32), in_=codes3[b][:].bitcast(I32)
            )

        nc.gpsimd.memset(wts_raw[:].bitcast(I32), 0)
        nc.vector.memset(rows[:], 0.0)
        nc.vector.memset(wfs[:].bitcast(I32), 0)
        make_identity(nc, identb[:])
        make_identity(nc, ident[:])
        nc.sync.dma_start(out=wt_raw[:].bitcast(I32), in_=w_t_words[0].bitcast(I32))
        nc.scalar.dma_start(out=gt[:], in_=g_t.rearrange("(p j) -> p j", j=4))
        for q in range(4):
            nc.scalar.dma_start(out=wts_raw[32 * q : 32 * q + 4, :].bitcast(I32), in_=w_t_scales[0, 4 * q : 4 * q + 4, :].bitcast(I32))
        nc.scalar.dma_start(out=bt16[:], in_=b_t.rearrange("(p j) -> p j", j=4))
        nc.scalar.dma_start(out=rows[0:4, :], in_=b_f.rearrange("(i p) -> i p", p=P))
        load_half(0)
        load_half(1)
        load_x(0)
        nc.scalar.dma_start(out=gc[:], in_=g_c.rearrange("(p j) -> p j", j=4))
        load_x(1)
        nc.sync.dma_start(out=wf[:].bitcast(I32), in_=w_f_words[0].bitcast(I32))
        for q in range(4):
            nc.scalar.dma_start(out=wfs[32 * q : 32 * q + 4, :].bitcast(I32), in_=w_f_scales[0, 4 * q : 4 * q + 4, :].bitcast(I32))
        load_x(2)
        vt = psum.tile([P, P], BF16, name="tp")

        with tc.manual_schedule():
            nc.vector.tensor_copy(out=wt[:].rearrange("p (j q e) -> p q j e", j=4, e=2), in_=wt_raw[:].rearrange("p (q j e) -> p q j e", j=4, e=2))
            mult(0, 0)
            interleave(0, 0, 96, "S")
            interleave(0, 96, 256, "V")
            nc.vector.tensor_copy(out=wts[:].rearrange("p (j q) -> p q j", j=4), in_=wts_raw[:].rearrange("p (q j) -> p q j", j=4))
            mult(0, 1)
            interleave(0, 256, 352, "S")
            nc.vector.tensor_copy(out=bt[:], in_=bt16[:])
            nc.vector.tensor_scalar_mul(out=nbt[:], in0=bt[:], scalar1=-1.0)
            interleave(0, 352, 512, "V")
            quant1(0, 0, 256)
            quant1(0, 256, 512)
            nc.tensor.transpose(vt[:], rows[:], identb[:])
            bias_res(0)
            bias_res(1)
            mx1(0)
            relu_s(0)
            res_v(0)
            res_g(0)
            mx1(1)
            relu_s(1)
            nc.vector.tensor_copy(out=bf[:], in_=vt[:, 0:4])
            trans_h(0, 0)
            trans_h(0, 1)
            for r in range(-3, B + 4):
                if 1 <= r + 1 < B:
                    interleave(r + 1, 0, 256, "S")
                if 0 <= 2 * r - 2 < U:
                    outs(2 * r - 2, 0)
                if 0 <= 2 * r - 1 < U:
                    mx2(2 * r - 1)
                if 2 <= 2 * r + 2 < U:
                    bias_res(2 * r + 2)
                if 0 <= 2 * r - 2 < U:
                    trans_r(2 * r - 2, 1)
                if 0 <= 2 * r < U:
                    quant2(2 * r)
                if 0 <= 2 * r - 4 < U:
                    trans_o(2 * r - 4, 0)
                if 1 <= r + 2 < B:
                    mult(r + 2, 1)
                if 0 <= 2 * r - 3 < U:
                    cast(2 * r - 3, 1)
                if 0 <= 2 * r - 2 < U:
                    outs(2 * r - 2, 1)
                if 1 <= 2 * r + 1 < U:
                    trans_h(2 * r + 1, 0)
                if 0 <= 2 * r - 1 < U:
                    relu2(2 * r - 1)
                if 1 <= 2 * r + 1 < U:
                    trans_h(2 * r + 1, 1)
                if 1 <= r + 1 < B:
                    quant1(r + 1)
                if 0 <= 2 * r < U:
                    mx2(2 * r)
                if 0 <= 2 * r + 1 < U:
                    hg(2 * r + 1, 1)
                if 2 <= 2 * r + 2 < U:
                    mx1(2 * r + 2)
                if 0 <= 2 * r - 4 < U:
                    pack_o(2 * r - 4)
                if 0 <= 2 * r - 3 < U:
                    trans_o(2 * r - 3, 0)
                if 0 <= 2 * r + 1 < U:
                    hg(2 * r + 1, 0)
                if 0 <= 2 * r - 3 < U:
                    trans_o(2 * r - 3, 1)
                if 0 <= 2 * r - 1 < U:
                    trans_r(2 * r - 1, 0)
                if 0 <= 2 * r < U:
                    relu2(2 * r)
                if 0 <= 2 * r - 1 < U:
                    trans_r(2 * r - 1, 1)
                if 1 <= 2 * r + 2 < U:
                    res_v(2 * r + 2)
                if 1 <= r + 2 < B:
                    mult(r + 2, 0)
                if 0 <= 2 * r - 3 < U:
                    pack_o(2 * r - 3)
                if 2 <= 2 * r + 2 < U:
                    relu_s(2 * r + 2)
                if 0 <= 2 * r - 2 < U:
                    cast(2 * r - 2, 1)
                if 0 <= 2 * r + 1 < U:
                    quant2(2 * r + 1)
                if 0 <= 2 * r - 1 < U:
                    outs(2 * r - 1, 0)
                if 2 <= 2 * r + 3 < U:
                    bias_res(2 * r + 3)
                if 2 <= 2 * r + 3 < U:
                    mx1(2 * r + 3)
                if 0 <= r - 2 < B:
                    quant3(r - 2)
                if 0 <= 2 * r - 2 < U:
                    cast(2 * r - 2, 0)
                if 2 <= 2 * r + 3 < U:
                    relu_s(2 * r + 3)
                if 0 <= 2 * r - 1 < U:
                    outs(2 * r - 1, 1)
                if 1 <= 2 * r + 2 < U:
                    trans_h(2 * r + 2, 1)
                if 1 <= r + 2 < B:
                    interleave(r + 2, 256, 512, "S")
                if 1 <= 2 * r + 3 < U:
                    res_v(2 * r + 3)
                if 1 <= 2 * r + 2 < U:
                    trans_h(2 * r + 2, 0)
                if 0 <= 2 * r - 2 < U:
                    trans_o(2 * r - 2, 1)
                if 0 <= 2 * r < U:
                    trans_r(2 * r, 0)
                if 0 <= 2 * r + 2 < U:
                    hg(2 * r + 2, 0)
                if 0 <= 2 * r - 1 < U:
                    cast(2 * r - 1, 0)
                if 0 <= 2 * r + 2 < U:
                    hg(2 * r + 2, 1)
                if 3 <= r + 5 < B:
                    load_x(r + 5)
                if 1 <= 2 * r + 3 < U:
                    res_g(2 * r + 3)
            for q in range(4):
                nc.scalar.dma_start(out=out_scales[0, 4 * q : 4 * q + 4, :].bitcast(I32), in_=sc3[32 * q : 32 * q + 4, :].bitcast(I32))
